import numpy as np
import ml_dtypes


def mxq(x, axis, fmt="e4m3"):
    dtype, down = {"e4m3": (ml_dtypes.float8_e4m3fn, 7), "e5m2": (ml_dtypes.float8_e5m2, 14)}[fmt]
    v = np.moveaxis(np.asarray(x, np.float32).astype(ml_dtypes.bfloat16).astype(np.float64), axis, -1)
    blocks = v.reshape(v.shape[:-1] + (-1, 32))
    amax = np.abs(blocks).max(-1, keepdims=True)
    byte = np.maximum(np.where(amax > 0, np.frexp(amax)[1] - 1 + 127, 0) - down, 1)
    scale = np.exp2(byte - 127.0)
    codes = (blocks / scale).astype(np.float32).astype(dtype).astype(np.float64)
    return np.moveaxis((codes * scale).reshape(v.shape), -1, axis)


WIDE = False


def mx_kscale(k):
    if not WIDE:
        return np.ones(k)
    levels = np.array([10, -10, 5, -5, 0])
    if k % 512:
        return np.exp2(np.random.permutation(np.resize(levels, k // 32))).repeat(32)
    a = np.empty((k // 512, 16))
    for p in range(k // 512):
        a[p, :8] = np.random.permutation(np.resize(levels, 8))
        for g in range(8):
            far = levels[np.abs(levels - a[p, g]) >= 10]
            a[p, g + 8] = far[np.random.randint(len(far))]
    return np.exp2(a.ravel()).repeat(32)


def f64(x):
    return np.asarray(x).astype(np.float64)


def striped(idx):
    return np.tile(idx.reshape(-1, 16).T, (8, 1)).astype(np.uint16)


def unstriped(offs):
    return offs[:16].T.reshape(-1).astype(np.int64)


E2M1 = np.array([0.0, 0.5, 1.0, 1.5, 2.0, 3.0, 4.0, 6.0, -0.0, -0.5, -1.0, -1.5, -2.0, -3.0, -4.0, -6.0])


def pack_weight(w, fmt):
    k, n = w.shape
    w = f64(np.asarray(w, np.float32).astype(ml_dtypes.bfloat16)).reshape(k // 32, 32, n)
    amax = np.abs(w).max(1)
    if fmt == "e4m3":
        byte = np.frexp(amax)[1] - 1 + 127 - 7
    else:
        mant, ex = np.frexp(amax / 6.0)
        byte = np.where(mant > 0.5, ex, ex - 1) + 127
    byte = np.clip(np.where(amax > 0, byte, 1), 1, 254)
    scaled = (w * np.exp2(127.0 - byte)[:, None, :]).reshape(k, n).astype(np.float32)
    by_word = np.ascontiguousarray(scaled.reshape(k // 512, 128, 4, n).transpose(0, 1, 3, 2))
    if fmt == "e4m3":
        words = by_word.astype(ml_dtypes.float8_e4m3fn).view(np.uint8)
    else:
        c = by_word.astype(ml_dtypes.float4_e2m1fn).view(np.uint8) & 0xF
        words = (c[..., 0::2] | (c[..., 1::2] << 4)).reshape(k // 512, 128, 2 * n)
    return np.ascontiguousarray(words), np.ascontiguousarray(byte.astype(np.uint8).reshape(k // 512, 16, n))


def unpack_weight(words, scales, fmt):
    g, _, n = scales.shape
    words = np.ascontiguousarray(words).reshape(g, 128, n, -1)
    if fmt == "e4m3":
        vals = words.view(ml_dtypes.float8_e4m3fn).astype(np.float64)
    else:
        nib = np.empty((g, 128, n, 4), np.uint8)
        nib[..., 0::2] = words & 0xF
        nib[..., 1::2] = words >> 4
        vals = E2M1[nib]
    vals = vals * np.repeat(np.exp2(scales.astype(np.float64) - 127.0), 8, axis=1)[..., None]
    return vals.transpose(0, 1, 3, 2).reshape(g * 512, n)


def relu(v):
    return np.maximum(v, 0.0)


K, T, E, C, H, N = 2048, 640, 4, 128, 512, 512


def by_expert(wq, xq):
    return np.concatenate([wq[e].T @ xq[:, e * C:(e + 1) * C] for e in range(E)], axis=1)


def setup_inputs():
    n = np.random.standard_normal
    s = mx_kscale(K)[:, None]
    u = mx_kscale(H)
    w1 = [pack_weight(m, "e2m1") for m in n((E, K, H)) / np.sqrt(K) / s[None] * u[None, None, :]]
    w2 = [pack_weight(m, "e2m1") for m in n((E, H, N)) / np.sqrt(H) / u[None, :, None]]
    return {
        "xT": (n((K, T)) * s).astype(np.float32),
        "w1_words": np.stack([m[0] for m in w1]),
        "w1_scales": np.stack([m[1] for m in w1]),
        "w2_words": np.stack([m[0] for m in w2]),
        "w2_scales": np.stack([m[1] for m in w2]),
        "gate": np.tile(np.random.uniform(0.2, 1.0, E * C), (N, 1)).astype(np.float32),
        "offs": striped(np.random.permutation(T)[:E * C]),
    }


def reference(xT, w1_words, w1_scales, w2_words, w2_scales, gate, offs):
    idx = unstriped(offs)
    w1 = np.stack([unpack_weight(w1_words[e], w1_scales[e], "e2m1") for e in range(E)])
    w2 = np.stack([unpack_weight(w2_words[e], w2_scales[e], "e2m1") for e in range(E)])
    xq = mxq(f64(xT)[:, idx], 0, "e4m3")
    h = relu(by_expert(w1, xq))
    y = by_expert(w2, mxq(h, 0, "e4m3"))
    out = np.zeros((N, T))
    out[:, idx] = f64(gate) * y
    return out

@@ -1,0 +1,260 @@
+from contextlib import ExitStack
+
+import concourse.mybir as mybir
+from concourse.masks import make_identity
+
+K, T, E, C, H, N = 2048, 640, 4, 128, 512, 512
+SLOTS = E * C
+FLOPS = 2 * SLOTS * H * (K + N)
+
+P = 128
+PACK = 4
+K_PASS = P * PACK
+PASSES = K // K_PASS
+W = 704
+OC = C // 16
+
+F32 = mybir.dt.float32
+BF16 = mybir.dt.bfloat16
+I32 = mybir.dt.int32
+U32 = mybir.dt.uint32
+U16 = mybir.dt.uint16
+U8 = mybir.dt.uint8
+FP8X4 = mybir.dt.float8_e4m3fn_x4
+FP4X4 = mybir.dt.float4_e2m1fn_x4
+COPY = mybir.ActivationFunctionType.Copy
+RELU = mybir.ActivationFunctionType.Relu
+MULT = mybir.AluOpType.mult
+
+HALF = T // 2
+CHUNKS = {0: ((0, HALF), (HALF, T)), 1: ((0, HALF), (HALF, T)), 2: ((0, HALF), (HALF, T)), 3: ((0, 384), (384, T))}
+CASTS = {
+    0: ((0, 320, "v"), (320, 480, "s"), (480, 640, "v")),
+    1: ((0, 320, "s"), (320, 640, "s")),
+    2: ((0, 320, "s"), (320, 640, "s")),
+    3: ((0, 256, "s"), (256, 384, "v"), (384, 512, "s"), (512, 640, "v")),
+}
+QUANTS = {
+    0: ((0, 256), (256, 512), (512, 640)),
+    1: ((0, 512), (512, 640)),
+    2: ((0, 512), (512, 640)),
+    3: ((0, 256), (256, 512), (512, 640)),
+}
+
+
+def tile_moe_pln_mlp_relu_kernel(
+    tc, xT, w1_words, w1_scales, w2_words, w2_scales, gate, offs, out
+):
+    nc = tc.nc
+    with ExitStack() as ctx:
+        keep = ctx.enter_context(tc.tile_pool(name="keep", bufs=1))
+        psum_a = ctx.enter_context(tc.psum_pool(name="psum_a", bufs=4))
+        psum_t = ctx.enter_context(tc.psum_pool(name="psum_t", bufs=2))
+        psum_y = ctx.enter_context(tc.psum_pool(name="psum_y", bufs=2))
+
+        offsets = keep.tile([P, SLOTS // 16], U16, name="offsets")
+
+        raw = [keep.tile([P, PACK, T], F32, name=f"raw{s}") for s in range(PASSES)]
+        grouped = [keep.tile([P, T * PACK], BF16, name=f"grouped{s}", align_bytes=64) for s in range(PASSES)]
+        words = [keep.tile([P, W], I32, name=f"words{s}", align_bytes=64) for s in range(PASSES)]
+        scales = {s: keep.tile([P, W], U8, name=f"scales{s}", align_bytes=64) for s in (0, 2, 3)}
+        slot_words = [keep.tile([P, SLOTS], U32, name=f"slot_words{s}", align_bytes=64) for s in range(PASSES)]
+        slot_scales = {s: keep.tile([P, SLOTS], U8, name=f"slot_scales{s}", align_bytes=64) for s in (0, 2, 3)}
+        shifted = keep.tile([P, SLOTS], U8, name="shifted", align_bytes=64)
+        w1w = [keep.tile([P, PASSES, 2 * H], U8, name=f"w1w{e}", align_bytes=64) for e in range(E)]
+        w1s_first = keep.tile([P, PASSES, H], U8, name="w1s_first", align_bytes=64)
+        w1s_rest = keep.tile([P, (E - 1) * PASSES, H], U8, name="w1s_rest", align_bytes=64)
+        w2w = keep.tile([P, E, 2 * N], U8, name="w2w", align_bytes=64)
+        w2s = keep.tile([P, E, N], U8, name="w2s", align_bytes=64)
+        gates = keep.tile([P, SLOTS], F32, name="gates")
+        outs = [keep.tile([P, T], F32, name=f"outs{b}") for b in range(N // P)]
+        ident = keep.tile([P, P], F32, name="ident")
+        dummy = keep.tile([P, 1], F32, name="dummy")
+
+        for s in range(PASSES):
+            for a, b in CHUNKS[s]:
+                nc.sync.dma_start(
+                    out=raw[s][:, :, a:b],
+                    in_=xT[s * K_PASS : (s + 1) * K_PASS, a:b].rearrange("(p j) t -> p j t", j=PACK),
+                )
+            if s == 0:
+                nc.sync.dma_start(offsets[:], offs)
+
+        nc.vector.memset(dummy[:], 0.0)
+        nc.scalar.activation(out=dummy[:], in_=dummy[:], func=RELU)
+        for s in range(PASSES):
+            nc.gpsimd.memset(words[s][:, T:W], 0)
+        for s in (0, 2, 3):
+            nc.gpsimd.memset(scales[s][:].bitcast(I32), 0)
+        nc.gpsimd.memset(shifted[:].bitcast(I32), 0)
+        make_identity(nc, ident[:])
+        for tile in (w1s_first, w2s, w1s_rest):
+            nc.gpsimd.memset(tile[:].rearrange("p s i -> p (s i)").bitcast(I32), 0)
+        for b in range(N // P):
+            nc.vector.memset(outs[b][:], 0.0)
+
+        def load_w1(e):
+            nc.sync.dma_start(out=w1w[e][:].bitcast(I32), in_=w1_words[e].rearrange("s p c -> p s c").bitcast(I32))
+
+        for r in range(4):
+            nc.sync.dma_start(
+                out=w1s_first[r:P:32, :, :].bitcast(I32),
+                in_=w1_scales[0, :, r:16:4, :].rearrange("s q i -> q s i").bitcast(I32),
+            )
+        load_w1(0)
+        for r in range(4):
+            nc.sync.dma_start(
+                out=w2s[r:P:32, :, :].bitcast(I32),
+                in_=w2_scales[:, 0, r:16:4, :].rearrange("e q i -> q e i").bitcast(I32),
+            )
+        nc.sync.dma_start(out=w2w[:].bitcast(I32), in_=w2_words[:, 0].rearrange("e p c -> p e c").bitcast(I32))
+        w1_rows = w1_scales[1:E].rearrange("e s q i -> (e s) q i")
+        for r in range(4):
+            nc.sync.dma_start(
+                out=w1s_rest[r:P:32, :, :].bitcast(I32),
+                in_=w1_rows[:, r:16:4, :].rearrange("g q i -> q g i").bitcast(I32),
+            )
+        load_w1(1)
+        nc.sync.dma_start(out=gates[:], in_=gate[0:P, :])
+        load_w1(2)
+        load_w1(3)
+
+        def cast(s):
+            for a, b, eng in CASTS[s]:
+                dst = grouped[s][:, a * PACK : b * PACK].rearrange("p (c i t) -> p c t i", i=4, t=PACK)
+                src = raw[s][:, :, a:b].rearrange("p t (c i) -> p c t i", i=4)
+                if eng == "v":
+                    nc.vector.tensor_copy(out=dst, in_=src)
+                else:
+                    nc.scalar.activation(out=dst, in_=src, func=COPY)
+
+        def quantize(s):
+            for a, b in QUANTS[s]:
+                nc.vector.quantize_mx(
+                    out=words[s][:, a:b].bitcast(FP8X4),
+                    scales=scales[0][4:P, a:b] if s == 1 else scales[s][:, a:b],
+                    in_=grouped[s][:, a * PACK : b * PACK],
+                )
+
+        def gather(s, e0, e1):
+            list_part = offsets[:, e0 * OC : e1 * OC]
+            nc.vector.tensor_copy(out=slot_words[s][:, e0 * C : e1 * C], in_=words[s][:].bitcast(U32).indirect(list_part))
+            if s >= 2:
+                gather_scales(s, e0, e1)
+
+        def gather_scales(s, e0, e1):
+            list_part = offsets[:, e0 * OC : e1 * OC]
+            nc.vector.tensor_copy(out=slot_scales[s][:, e0 * C : e1 * C], in_=scales[s][:].indirect(list_part))
+
+        acc = {}
+
+        def layer1(e, s):
+            if s == 0:
+                acc[e] = psum_a.tile([P, H], F32, name="a")
+            cols = slice(e * C, (e + 1) * C)
+            nc.tensor.matmul_mx(
+                out=acc[e][:],
+                lhsT=slot_words[s][:, cols].bitcast(FP8X4),
+                lhsT_scale=shifted[:, cols] if s == 1 else slot_scales[s][:, cols],
+                rhs=w1w[e][:, s, :].bitcast(FP4X4),
+                rhs_scale=(w1s_first[:, s, :] if e == 0 else w1s_rest[:, (e - 1) * PASSES + s, :]),
+                start=(s == 0),
+                stop=(s == 3),
+            )
+
+        h_rows, h_grouped, h_words, h_scales, y_rows = {}, {}, {}, {}, {}
+
+        def hidden(e):
+            h_rows[e] = keep.tile([P, H], BF16, name=f"h_rows{e}")
+            nc.scalar.activation(
+                out=h_rows[e][:].rearrange("p (u m v) -> p u m v", u=2, v=2),
+                in_=acc[e][:].rearrange("p (m u v) -> p u m v", u=2, v=2),
+                func=RELU,
+            )
+            turned = psum_t.tile([P, 2, C], F32, name="turned")
+            pairs = h_rows[e][:].bitcast(F32)
+            for u in range(2):
+                nc.tensor.transpose(turned[:, u, :], pairs[:, u * P : (u + 1) * P], ident[:])
+            h_grouped[e] = keep.tile([P, C * PACK], BF16, name=f"h_grouped{e}", align_bytes=64)
+            nc.scalar.copy(
+                out=h_grouped[e][:].bitcast(F32).rearrange("p (c u) -> p c u", u=2),
+                in_=turned[:].rearrange("p u c -> p c u"),
+            )
+
+        def hidden_quantize(e):
+            h_words[e] = keep.tile([P, C], U32, name=f"h_words{e}", align_bytes=64)
+            h_scales[e] = keep.tile([P, C], U8, name=f"h_scales{e}", align_bytes=64)
+            nc.vector.quantize_mx(out=h_words[e][:].bitcast(FP8X4), scales=h_scales[e][:], in_=h_grouped[e][:])
+
+        def layer2(e):
+            y = psum_y.tile([P, N // P, C], F32, name="y")
+            for b in range(N // P):
+                nc.tensor.matmul_mx(
+                    out=y[:, b, :],
+                    lhsT=w2w[:, e, b * 2 * P : (b + 1) * 2 * P].bitcast(FP4X4),
+                    lhsT_scale=w2s[:, e, b * P : (b + 1) * P],
+                    rhs=h_words[e][:].bitcast(FP8X4),
+                    rhs_scale=h_scales[e][:],
+                    start=True,
+                    stop=True,
+                )
+            return y
+
+        y_first = [keep.tile([P, N // P, C], F32, name=f"y_first{e}") for e in range(2)]
+        y_last = keep.tile([P, N // P, 2 * C], F32, name="y_last")
+
+        def leave(e, y):
+            if e < 2:
+                nc.scalar.activation(out=y_first[e][:], in_=y[:], func=COPY)
+            else:
+                nc.scalar.activation(out=y_last[:, :, (e - 2) * C : (e - 1) * C], in_=y[:], func=COPY)
+
+        def scatter(b, e0, e1, y):
+            nc.vector.tensor_tensor(
+                outs[b][:].indirect(offsets[:, e0 * OC : e1 * OC]), y, gates[:, e0 * C : e1 * C], MULT
+            )
+
+        for s in range(2):
+            cast(s)
+            quantize(s)
+            gather(s, 0, E)
+        gather_scales(0, 0, E)
+        cast(2)
+        nc.scalar.dma_start(out=shifted[0:100, :].bitcast(I32), in_=slot_scales[0][4:104, :].bitcast(I32))
+        quantize(2)
+        gather(2, 0, 1)
+        cast(3)
+        quantize(3)
+        gather(3, 0, 1)
+        for s in range(PASSES):
+            layer1(0, s)
+        hidden(0)
+        gather(2, 1, 2)
+        gather(3, 1, 2)
+        for s in range(PASSES):
+            layer1(1, s)
+        hidden(1)
+        gather(2, 2, 4)
+        for e in (2, 3):
+            for s in range(2):
+                layer1(e, s)
+        hidden_quantize(0)
+        leave(0, layer2(0))
+        gather(3, 2, 4)
+        hidden_quantize(1)
+        leave(1, layer2(1))
+        for e in (2, 3):
+            for s in (2, 3):
+                layer1(e, s)
+            hidden(e)
+        for b in range(N // P):
+            scatter(b, 0, 1, y_first[0][:, b, :])
+        hidden_quantize(2)
+        hidden_quantize(3)
+        leave(2, layer2(2))
+        leave(3, layer2(3))
+        for b in range(N // P):
+            scatter(b, 1, 2, y_first[1][:, b, :])
+        for b in range(N // P):
+            scatter(b, 2, 4, y_last[:, b, :])
+            nc.sync.dma_start(out=out[b * P : (b + 1) * P, :], in_=outs[b][:])

@@ -13,6 +13,8 @@ K_PASS = P * PACK
 PASSES = K // K_PASS
 W = 704
 OC = C // 16
+BLOCKS = N // P
+SPARE = C
 
 F32 = mybir.dt.float32
 BF16 = mybir.dt.bfloat16
@@ -26,16 +28,15 @@ COPY = mybir.ActivationFunctionType.Copy
 RELU = mybir.ActivationFunctionType.Relu
 MULT = mybir.AluOpType.mult
 
-HALF = T // 2
-CHUNKS = {0: ((0, HALF), (HALF, T)), 1: ((0, HALF), (HALF, T)), 2: ((0, HALF), (HALF, T)), 3: ((0, 384), (384, T))}
 CASTS = {
-    0: ((0, 320, "v"), (320, 480, "s"), (480, 640, "v")),
-    1: ((0, 320, "s"), (320, 640, "s")),
-    2: ((0, 320, "s"), (320, 640, "s")),
-    3: ((0, 256, "s"), (256, 384, "v"), (384, 512, "s"), (512, 640, "v")),
+    0: ((0, 384, "v"), (384, 640, "s")),
+    1: ((0, 512, "s"), (512, 640, "s")),
+    2: ((0, 512, "s"), (512, 640, "s")),
+    3: ((0, 256, "s"), (256, 512, "s"), (512, 640, "s")),
 }
+Y_BANKS = (("y0_0", "y0_1"), ("y1_0", "y1_1"), ("a0", "a1"), ("t", "y3_1"))
 QUANTS = {
-    0: ((0, 256), (256, 512), (512, 640)),
+    0: ((0, 256), (256, 384), (384, 640)),
     1: ((0, 512), (512, 640)),
     2: ((0, 512), (512, 640)),
     3: ((0, 256), (256, 512), (512, 640)),
@@ -48,80 +49,71 @@ def tile_moe_pln_mlp_relu_kernel(
     nc = tc.nc
     with ExitStack() as ctx:
         keep = ctx.enter_context(tc.tile_pool(name="keep", bufs=1))
-        psum_a = ctx.enter_context(tc.psum_pool(name="psum_a", bufs=4))
-        psum_t = ctx.enter_context(tc.psum_pool(name="psum_t", bufs=2))
-        psum_y = ctx.enter_context(tc.psum_pool(name="psum_y", bufs=2))
+        psum = ctx.enter_context(tc.psum_pool(name="psum", bufs=1))
 
         offsets = keep.tile([P, SLOTS // 16], U16, name="offsets")
 
         raw = [keep.tile([P, PACK, T], F32, name=f"raw{s}") for s in range(PASSES)]
-        grouped = [keep.tile([P, T * PACK], BF16, name=f"grouped{s}", align_bytes=64) for s in range(PASSES)]
         words = [keep.tile([P, W], I32, name=f"words{s}", align_bytes=64) for s in range(PASSES)]
-        scales = {s: keep.tile([P, W], U8, name=f"scales{s}", align_bytes=64) for s in (0, 2, 3)}
-        slot_words = [keep.tile([P, SLOTS], U32, name=f"slot_words{s}", align_bytes=64) for s in range(PASSES)]
-        slot_scales = {s: keep.tile([P, SLOTS], U8, name=f"slot_scales{s}", align_bytes=64) for s in (0, 2, 3)}
-        shifted = keep.tile([P, SLOTS], U8, name="shifted", align_bytes=64)
-        w1w = [keep.tile([P, PASSES, 2 * H], U8, name=f"w1w{e}", align_bytes=64) for e in range(E)]
-        w1s_first = keep.tile([P, PASSES, H], U8, name="w1s_first", align_bytes=64)
-        w1s_rest = keep.tile([P, (E - 1) * PASSES, H], U8, name="w1s_rest", align_bytes=64)
-        w2w = keep.tile([P, E, 2 * N], U8, name="w2w", align_bytes=64)
+        scales = [keep.tile([P, W], U8, name=f"scales{s}", align_bytes=64) for s in range(PASSES)]
+        w1w_first = [keep.tile([P, 2, 2 * H], U8, name=f"w1w_first{u}", align_bytes=64) for u in range(2)]
+        w1w_rest = [keep.tile([P, PASSES, 2 * H], U8, name=f"w1w_rest{e}", align_bytes=64) for e in range(1, E)]
+        w1s = [keep.tile([P, 2 * PASSES, H], U8, name=f"w1s{u}", align_bytes=64) for u in range(2)]
+        w2w_first = keep.tile([P, 2 * N], U8, name="w2w_first", align_bytes=64)
+        w2w_rest = keep.tile([P, E - 1, 2 * N], U8, name="w2w_rest", align_bytes=64)
         w2s = keep.tile([P, E, N], U8, name="w2s", align_bytes=64)
         gates = keep.tile([P, SLOTS], F32, name="gates")
-        outs = [keep.tile([P, T], F32, name=f"outs{b}") for b in range(N // P)]
+        outs = [keep.tile([P, T + SPARE], F32, name=f"outs{b}", align_bytes=64) for b in range(BLOCKS)]
         ident = keep.tile([P, P], F32, name="ident")
-        dummy = keep.tile([P, 1], F32, name="dummy")
+        zero = keep.tile([P, 1], F32, name="zero")
 
         for s in range(PASSES):
-            for a, b in CHUNKS[s]:
-                nc.sync.dma_start(
-                    out=raw[s][:, :, a:b],
-                    in_=xT[s * K_PASS : (s + 1) * K_PASS, a:b].rearrange("(p j) t -> p j t", j=PACK),
-                )
+            nc.sync.dma_start(
+                out=raw[s][:], in_=xT[s * K_PASS : (s + 1) * K_PASS, :].rearrange("(p j) t -> p j t", j=PACK)
+            )
             if s == 0:
                 nc.sync.dma_start(offsets[:], offs)
 
-        nc.vector.memset(dummy[:], 0.0)
-        nc.scalar.activation(out=dummy[:], in_=dummy[:], func=RELU)
-        for s in range(PASSES):
-            nc.gpsimd.memset(words[s][:, T:W], 0)
-        for s in (0, 2, 3):
-            nc.gpsimd.memset(scales[s][:].bitcast(I32), 0)
-        nc.gpsimd.memset(shifted[:].bitcast(I32), 0)
+        nc.vector.memset(zero[:], 0.0)
+        for b in range(1, BLOCKS):
+            nc.scalar.activation(out=outs[b][:, 0:T], in_=zero[:].to_broadcast([P, T]), func=COPY)
         make_identity(nc, ident[:])
-        for tile in (w1s_first, w2s, w1s_rest):
+        for tile in (w2s, w1s[1]):
             nc.gpsimd.memset(tile[:].rearrange("p s i -> p (s i)").bitcast(I32), 0)
-        for b in range(N // P):
-            nc.vector.memset(outs[b][:], 0.0)
+        nc.vector.memset(w1s[0][:].rearrange("p s i -> p (s i)").bitcast(I32), 0)
+        for s in range(PASSES):
+            nc.vector.memset(words[s][:, T:W], 0)
+            nc.vector.memset(scales[s][:].bitcast(I32), 0)
+        nc.vector.memset(outs[0][:, 0:T], 0.0)
 
-        def load_w1(e):
-            nc.sync.dma_start(out=w1w[e][:].bitcast(I32), in_=w1_words[e].rearrange("s p c -> p s c").bitcast(I32))
+        def load_scale_rows(tile, rows):
+            for r in range(4):
+                nc.sync.dma_start(
+                    out=tile[r:P:32, :, :].bitcast(I32), in_=rows[:, r:16:4, :].rearrange("g q i -> q g i").bitcast(I32)
+                )
 
-        for r in range(4):
-            nc.sync.dma_start(
-                out=w1s_first[r:P:32, :, :].bitcast(I32),
-                in_=w1_scales[0, :, r:16:4, :].rearrange("s q i -> q s i").bitcast(I32),
-            )
-        load_w1(0)
-        for r in range(4):
-            nc.sync.dma_start(
-                out=w2s[r:P:32, :, :].bitcast(I32),
-                in_=w2_scales[:, 0, r:16:4, :].rearrange("e q i -> q e i").bitcast(I32),
-            )
-        nc.sync.dma_start(out=w2w[:].bitcast(I32), in_=w2_words[:, 0].rearrange("e p c -> p e c").bitcast(I32))
-        w1_rows = w1_scales[1:E].rearrange("e s q i -> (e s) q i")
-        for r in range(4):
-            nc.sync.dma_start(
-                out=w1s_rest[r:P:32, :, :].bitcast(I32),
-                in_=w1_rows[:, r:16:4, :].rearrange("g q i -> q g i").bitcast(I32),
-            )
-        load_w1(1)
+        def load_words(tile, rows):
+            nc.sync.dma_start(out=tile[:].bitcast(I32), in_=rows.rearrange("g p c -> p g c").bitcast(I32))
+
+        load_scale_rows(w1s[0], w1_scales[0:2].rearrange("e s q i -> (e s) q i"))
+        for u in range(2):
+            load_words(w1w_first[u], w1_words[0, 2 * u : 2 * u + 2])
+        load_words(w1w_rest[0], w1_words[1])
+        load_scale_rows(w2s, w2_scales[:, 0])
+        nc.sync.dma_start(out=w2w_first[:].bitcast(I32), in_=w2_words[0, 0].bitcast(I32))
         nc.sync.dma_start(out=gates[:], in_=gate[0:P, :])
-        load_w1(2)
-        load_w1(3)
+        load_words(w2w_rest, w2_words[1:E, 0])
+        load_scale_rows(w1s[1], w1_scales[2:E].rearrange("e s q i -> (e s) q i"))
+        for e in range(2, E):
+            load_words(w1w_rest[e - 1], w1_words[e])
+
+        grouped = {}
 
         def cast(s):
             for a, b, eng in CASTS[s]:
-                dst = grouped[s][:, a * PACK : b * PACK].rearrange("p (c i t) -> p c t i", i=4, t=PACK)
+                tag = f"scales{s - 1}" if eng == "v" and s > 0 else f"grouped{s}_{a}"
+                grouped[s, a, b] = keep.tile([P, (b - a) * PACK], BF16, name=f"grouped{s}_{a}", tag=tag, align_bytes=64)
+                dst = grouped[s, a, b][:].rearrange("p (c i t) -> p c t i", i=4, t=PACK)
                 src = raw[s][:, :, a:b].rearrange("p t (c i) -> p c t i", i=4)
                 if eng == "v":
                     nc.vector.tensor_copy(out=dst, in_=src)
@@ -130,131 +122,144 @@ def tile_moe_pln_mlp_relu_kernel(
 
         def quantize(s):
             for a, b in QUANTS[s]:
+                a0, b0 = [(c, d) for c, d, eng in CASTS[s] if c <= a and b <= d][0]
                 nc.vector.quantize_mx(
                     out=words[s][:, a:b].bitcast(FP8X4),
-                    scales=scales[0][4:P, a:b] if s == 1 else scales[s][:, a:b],
-                    in_=grouped[s][:, a * PACK : b * PACK],
+                    scales=scales[s][:, a:b],
+                    in_=grouped[s, a0, b0][:, (a - a0) * PACK : (b - a0) * PACK],
                 )
 
-        def gather(s, e0, e1):
-            list_part = offsets[:, e0 * OC : e1 * OC]
-            nc.vector.tensor_copy(out=slot_words[s][:, e0 * C : e1 * C], in_=words[s][:].bitcast(U32).indirect(list_part))
-            if s >= 2:
-                gather_scales(s, e0, e1)
+        slot_words, slot_scales = {}, {}
+
+        def gather(kind, s, e0, e1, dst):
+            src = words[s][:].bitcast(U32) if kind is slot_words else scales[s][:]
+            nc.vector.tensor_copy(out=dst, in_=src.indirect(offsets[:, e0 * OC : e1 * OC]))
+            for e in range(e0, e1):
+                kind[s, e] = dst[:, (e - e0) * C : (e - e0 + 1) * C]
+
+        def gather_words(s, e0, e1, tag=None):
+            name = f"slot_words{s}_{e0}"
+            dst = keep.tile([P, (e1 - e0) * C], U32, name=name, tag=tag or name, align_bytes=64)
+            gather(slot_words, s, e0, e1, dst[:])
 
         def gather_scales(s, e0, e1):
-            list_part = offsets[:, e0 * OC : e1 * OC]
-            nc.vector.tensor_copy(out=slot_scales[s][:, e0 * C : e1 * C], in_=scales[s][:].indirect(list_part))
+            dst = keep.tile([P, (e1 - e0) * C], U8, name=f"slot_scales{s}_{e0}", align_bytes=64)
+            gather(slot_scales, s, e0, e1, dst[:])
 
         acc = {}
 
         def layer1(e, s):
             if s == 0:
-                acc[e] = psum_a.tile([P, H], F32, name="a")
-            cols = slice(e * C, (e + 1) * C)
+                acc[e] = psum.tile([P, H], F32, name=f"a{e}", tag=f"a{e}" if e < 2 else f"y{e - 2}_1")
             nc.tensor.matmul_mx(
                 out=acc[e][:],
-                lhsT=slot_words[s][:, cols].bitcast(FP8X4),
-                lhsT_scale=shifted[:, cols] if s == 1 else slot_scales[s][:, cols],
-                rhs=w1w[e][:, s, :].bitcast(FP4X4),
-                rhs_scale=(w1s_first[:, s, :] if e == 0 else w1s_rest[:, (e - 1) * PASSES + s, :]),
+                lhsT=slot_words[s, e].bitcast(FP8X4),
+                lhsT_scale=slot_scales[s, e],
+                rhs=(w1w_first[s // 2][:, s % 2, :] if e == 0 else w1w_rest[e - 1][:, s, :]).bitcast(FP4X4),
+                rhs_scale=w1s[e // 2][:, (e % 2) * PASSES + s, :],
                 start=(s == 0),
-                stop=(s == 3),
+                stop=(s == (2 if e == 1 else 3)),
             )
 
-        h_rows, h_grouped, h_words, h_scales, y_rows = {}, {}, {}, {}, {}
+        h_homes, h_words, h_scales, y_rows = {}, {}, {}, {}
 
         def hidden(e):
-            h_rows[e] = keep.tile([P, H], BF16, name=f"h_rows{e}")
+            h_rows = keep.tile([P, H], BF16, name=f"h_rows{e}", align_bytes=64)
             nc.scalar.activation(
-                out=h_rows[e][:].rearrange("p (u m v) -> p u m v", u=2, v=2),
+                out=h_rows[:].rearrange("p (u m v) -> p u m v", u=2, v=2),
                 in_=acc[e][:].rearrange("p (m u v) -> p u m v", u=2, v=2),
                 func=RELU,
             )
-            turned = psum_t.tile([P, 2, C], F32, name="turned")
-            pairs = h_rows[e][:].bitcast(F32)
+            turned = psum.tile([P, 2, C], F32, name=f"turned{e}", tag="t" if e == 0 else Y_BANKS[e - 1][0])
+            pairs = h_rows[:].bitcast(F32)
             for u in range(2):
                 nc.tensor.transpose(turned[:, u, :], pairs[:, u * P : (u + 1) * P], ident[:])
-            h_grouped[e] = keep.tile([P, C * PACK], BF16, name=f"h_grouped{e}", align_bytes=64)
-            nc.scalar.copy(
-                out=h_grouped[e][:].bitcast(F32).rearrange("p (c u) -> p c u", u=2),
-                in_=turned[:].rearrange("p u c -> p c u"),
-            )
+            if e == 0:
+                first = keep.tile([P, 2 * C], F32, name="h_first", tag="h_first", align_bytes=64)
+                h_homes[e] = [(0, C, first[:])]
+            else:
+                b0 = 2 * (e % 2)
+                h_homes[e] = [(0, C // 2, outs[b0][:, T:]), (C // 2, C, outs[b0 + 1][:, T:])]
+            for a, b, home in h_homes[e]:
+                nc.scalar.copy(
+                    out=home.rearrange("p (c u) -> p c u", u=2), in_=turned[:, :, a:b].rearrange("p u c -> p c u")
+                )
 
         def hidden_quantize(e):
             h_words[e] = keep.tile([P, C], U32, name=f"h_words{e}", align_bytes=64)
             h_scales[e] = keep.tile([P, C], U8, name=f"h_scales{e}", align_bytes=64)
-            nc.vector.quantize_mx(out=h_words[e][:].bitcast(FP8X4), scales=h_scales[e][:], in_=h_grouped[e][:])
+            for a, b, home in h_homes[e]:
+                nc.vector.quantize_mx(
+                    out=h_words[e][:, a:b].bitcast(FP8X4), scales=h_scales[e][:, a:b], in_=home.bitcast(BF16)
+                )
 
         def layer2(e):
-            y = psum_y.tile([P, N // P, C], F32, name="y")
-            for b in range(N // P):
-                nc.tensor.matmul_mx(
-                    out=y[:, b, :],
-                    lhsT=w2w[:, e, b * 2 * P : (b + 1) * 2 * P].bitcast(FP4X4),
-                    lhsT_scale=w2s[:, e, b * P : (b + 1) * P],
-                    rhs=h_words[e][:].bitcast(FP8X4),
-                    rhs_scale=h_scales[e][:],
-                    start=True,
-                    stop=True,
-                )
-            return y
+            w2 = w2w_first[:] if e == 0 else w2w_rest[:, e - 1, :]
+            y_rows[e] = keep.tile([P, BLOCKS * C], F32, name=f"y_rows{e}")
+            first = 2 * (e % 2)
+            for half, b0 in enumerate((first, 2 - first)):
+                y = psum.tile([P, 2 * C], F32, name=f"y{e}_{half}", tag=Y_BANKS[e][half])
+                for b in (b0, b0 + 1):
+                    nc.tensor.matmul_mx(
+                        out=y[:, (b - b0) * C : (b - b0 + 1) * C],
+                        lhsT=w2[:, b * 2 * P : (b + 1) * 2 * P].bitcast(FP4X4),
+                        lhsT_scale=w2s[:, e, b * P : (b + 1) * P],
+                        rhs=h_words[e][:].bitcast(FP8X4),
+                        rhs_scale=h_scales[e][:],
+                        start=True,
+                        stop=True,
+                    )
+                nc.scalar.activation(out=y_rows[e][:, b0 * C : (b0 + 2) * C], in_=y[:], func=COPY)
 
-        y_first = [keep.tile([P, N // P, C], F32, name=f"y_first{e}") for e in range(2)]
-        y_last = keep.tile([P, N // P, 2 * C], F32, name="y_last")
-
-        def leave(e, y):
-            if e < 2:
-                nc.scalar.activation(out=y_first[e][:], in_=y[:], func=COPY)
-            else:
-                nc.scalar.activation(out=y_last[:, :, (e - 2) * C : (e - 1) * C], in_=y[:], func=COPY)
-
-        def scatter(b, e0, e1, y):
+        def scatter(e, b):
             nc.vector.tensor_tensor(
-                outs[b][:].indirect(offsets[:, e0 * OC : e1 * OC]), y, gates[:, e0 * C : e1 * C], MULT
+                outs[b][:].indirect(offsets[:, e * OC : (e + 1) * OC]),
+                y_rows[e][:, b * C : (b + 1) * C],
+                gates[:, e * C : (e + 1) * C],
+                MULT,
             )
+            if e == E - 1:
+                nc.sync.dma_start(out=out[b * P : (b + 1) * P, :], in_=outs[b][:, 0:T])
 
-        for s in range(2):
-            cast(s)
-            quantize(s)
-            gather(s, 0, E)
+        cast(0)
+        quantize(0)
+        gather_words(0, 0, E)
         gather_scales(0, 0, E)
+        cast(1)
+        quantize(1)
+        gather_words(1, 0, 2)
+        gather_scales(1, 0, E)
         cast(2)
-        nc.scalar.dma_start(out=shifted[0:100, :].bitcast(I32), in_=slot_scales[0][4:104, :].bitcast(I32))
         quantize(2)
-        gather(2, 0, 1)
+        gather_words(2, 0, 1)
+        gather_scales(2, 0, E)
         cast(3)
         quantize(3)
-        gather(3, 0, 1)
+        for e0, e1 in ((0, 1), (1, 2), (2, E)):
+            gather_words(3, e0, e1)
+            gather_scales(3, e0, e1)
         for s in range(PASSES):
             layer1(0, s)
         hidden(0)
-        gather(2, 1, 2)
-        gather(3, 1, 2)
-        for s in range(PASSES):
+        gather_words(2, 1, 2, tag="h_rows0")
+        for s in (0, 1, 3, 2):
             layer1(1, s)
-        hidden(1)
-        gather(2, 2, 4)
-        for e in (2, 3):
-            for s in range(2):
-                layer1(e, s)
         hidden_quantize(0)
-        leave(0, layer2(0))
-        gather(3, 2, 4)
-        hidden_quantize(1)
-        leave(1, layer2(1))
-        for e in (2, 3):
-            for s in (2, 3):
-                layer1(e, s)
-            hidden(e)
-        for b in range(N // P):
-            scatter(b, 0, 1, y_first[0][:, b, :])
-        hidden_quantize(2)
-        hidden_quantize(3)
-        leave(2, layer2(2))
-        leave(3, layer2(3))
-        for b in range(N // P):
-            scatter(b, 1, 2, y_first[1][:, b, :])
-        for b in range(N // P):
-            scatter(b, 2, 4, y_last[:, b, :])
-            nc.sync.dma_start(out=out[b * P : (b + 1) * P, :], in_=outs[b][:])
+        late = keep.tile([P, 4 * C], U32, name="late_words", tag="h_first", align_bytes=64)
+        gather(slot_words, 1, 2, E, late[:, 0 : 2 * C])
+        gather(slot_words, 2, 2, E, late[:, 2 * C : 4 * C])
+        layer2(0)
+        for e in range(E):
+            first = 2 * (e % 2)
+            if e + 1 < E:
+                hidden(e + 1)
+            scatter(e, first)
+            scatter(e, first + 1)
+            if e + 2 < E:
+                for s in range(PASSES):
+                    layer1(e + 2, s)
+            if e + 1 < E:
+                hidden_quantize(e + 1)
+                layer2(e + 1)
+            scatter(e, 2 - first)
+            scatter(e, 3 - first)

@@ -29,16 +29,19 @@ RELU = mybir.ActivationFunctionType.Relu
 MULT = mybir.AluOpType.mult
 
 CASTS = {
-    0: ((0, 384, "v"), (384, 640, "s")),
-    1: ((0, 512, "s"), (512, 640, "s")),
-    2: ((0, 512, "s"), (512, 640, "s")),
-    3: ((0, 256, "s"), (256, 512, "s"), (512, 640, "s")),
+    0: ((0, 384, "v"), (384, 512, "v"), (512, 640, "s")),
+    1: ((0, 256, "s"), (256, 384, "s"), (384, 640, "v")),
+    2: ((0, 512, "s"), (512, 640, "v")),
+    3: ((0, 256, "v"), (256, 512, "s"), (512, 640, "s")),
 }
-Y_BANKS = (("y0_0", "y0_1"), ("y1_0", "y1_1"), ("a0", "a1"), ("t", "y3_1"))
+Y_BANKS = (("y0_0", "y0_1"), ("y1_0", "y1_1"), ("a0", "a1"), ("t0", "y0_1"))
+PASS_ORDER = ((0, 1, 2, 3), (3, 0, 1, 2), (0, 1, 2, 3), (0, 1, 2, 3))
+CAST_AFTER = (None, "words0", "words1", "grouped2_0")
+CHUNKS = (((0, 384), (384, T)), ((0, T),), ((0, T),), ((0, T),))
 QUANTS = {
-    0: ((0, 256), (256, 384), (384, 640)),
-    1: ((0, 512), (512, 640)),
-    2: ((0, 512), (512, 640)),
+    0: ((0, 256), (256, 384), (384, 512), (512, 640)),
+    1: ((0, 256), (384, 640), (256, 384)),
+    2: ((512, 640), (0, 512)),
     3: ((0, 256), (256, 512), (512, 640)),
 }
 
@@ -55,36 +58,18 @@ def tile_moe_pln_mlp_relu_kernel(
 
         raw = [keep.tile([P, PACK, T], F32, name=f"raw{s}") for s in range(PASSES)]
         words = [keep.tile([P, W], I32, name=f"words{s}", align_bytes=64) for s in range(PASSES)]
-        scales = [keep.tile([P, W], U8, name=f"scales{s}", align_bytes=64) for s in range(PASSES)]
+        scales = {s: keep.tile([P, W], U8, name=f"scales{s}", align_bytes=64) for s in (0, 2, 3)}
+        shifted = keep.tile([P, SLOTS], U8, name="shifted", align_bytes=64)
         w1w_first = [keep.tile([P, 2, 2 * H], U8, name=f"w1w_first{u}", align_bytes=64) for u in range(2)]
         w1w_rest = [keep.tile([P, PASSES, 2 * H], U8, name=f"w1w_rest{e}", align_bytes=64) for e in range(1, E)]
-        w1s = [keep.tile([P, 2 * PASSES, H], U8, name=f"w1s{u}", align_bytes=64) for u in range(2)]
-        w2w_first = keep.tile([P, 2 * N], U8, name="w2w_first", align_bytes=64)
-        w2w_rest = keep.tile([P, E - 1, 2 * N], U8, name="w2w_rest", align_bytes=64)
+        w1s = [keep.tile([P, PASSES, H], U8, name=f"w1s{e}", align_bytes=64) for e in range(E)]
+        w2w = [keep.tile([P, 1, 2 * N], U8, name=f"w2w{e}", align_bytes=64) for e in range(2)]
+        w2w_late = keep.tile([P, 2, 2 * N], U8, name="w2w_late", align_bytes=64)
         w2s = keep.tile([P, E, N], U8, name="w2s", align_bytes=64)
         gates = keep.tile([P, SLOTS], F32, name="gates")
         outs = [keep.tile([P, T + SPARE], F32, name=f"outs{b}", align_bytes=64) for b in range(BLOCKS)]
         ident = keep.tile([P, P], F32, name="ident")
         zero = keep.tile([P, 1], F32, name="zero")
-
-        for s in range(PASSES):
-            nc.sync.dma_start(
-                out=raw[s][:], in_=xT[s * K_PASS : (s + 1) * K_PASS, :].rearrange("(p j) t -> p j t", j=PACK)
-            )
-            if s == 0:
-                nc.sync.dma_start(offsets[:], offs)
-
-        nc.vector.memset(zero[:], 0.0)
-        for b in range(1, BLOCKS):
-            nc.scalar.activation(out=outs[b][:, 0:T], in_=zero[:].to_broadcast([P, T]), func=COPY)
-        make_identity(nc, ident[:])
-        for tile in (w2s, w1s[1]):
-            nc.gpsimd.memset(tile[:].rearrange("p s i -> p (s i)").bitcast(I32), 0)
-        nc.vector.memset(w1s[0][:].rearrange("p s i -> p (s i)").bitcast(I32), 0)
-        for s in range(PASSES):
-            nc.vector.memset(words[s][:, T:W], 0)
-            nc.vector.memset(scales[s][:].bitcast(I32), 0)
-        nc.vector.memset(outs[0][:, 0:T], 0.0)
 
         def load_scale_rows(tile, rows):
             for r in range(4):
@@ -92,26 +77,51 @@ def tile_moe_pln_mlp_relu_kernel(
                     out=tile[r:P:32, :, :].bitcast(I32), in_=rows[:, r:16:4, :].rearrange("g q i -> q g i").bitcast(I32)
                 )
 
+        for eng, tile in ((nc.gpsimd, w1s[0]), (nc.vector, w2s), (nc.gpsimd, w1s[1]), (nc.gpsimd, w1s[2]), (nc.gpsimd, w1s[3])):
+            eng.memset(tile[:].rearrange("p s i -> p (s i)").bitcast(I32), 0)
+        for s in range(PASSES):
+            if s == PASSES - 1:
+                load_scale_rows(w1s[0], w1_scales[0])
+            for a, b in CHUNKS[s]:
+                nc.sync.dma_start(
+                    out=raw[s][:, :, a:b],
+                    in_=xT[s * K_PASS : (s + 1) * K_PASS, a:b].rearrange("(p j) t -> p j t", j=PACK),
+                )
+            if s == 0:
+                nc.sync.dma_start(offsets[:], offs)
+
+        nc.vector.memset(zero[:], 0.0)
+        for b in range(1, BLOCKS):
+            nc.scalar.activation(out=outs[b][:, 0:T], in_=zero[:].to_broadcast([P, T]), func=COPY)
+        make_identity(nc, ident[:])
+        for s in range(PASSES):
+            nc.vector.memset(words[s][:, T:W], 0)
+        for tile in (scales[0], scales[2], scales[3], shifted):
+            nc.vector.memset(tile[:].bitcast(I32), 0)
+        nc.vector.memset(outs[0][:, 0:T], 0.0)
+
         def load_words(tile, rows):
             nc.sync.dma_start(out=tile[:].bitcast(I32), in_=rows.rearrange("g p c -> p g c").bitcast(I32))
 
-        load_scale_rows(w1s[0], w1_scales[0:2].rearrange("e s q i -> (e s) q i"))
         for u in range(2):
             load_words(w1w_first[u], w1_words[0, 2 * u : 2 * u + 2])
-        load_words(w1w_rest[0], w1_words[1])
         load_scale_rows(w2s, w2_scales[:, 0])
-        nc.sync.dma_start(out=w2w_first[:].bitcast(I32), in_=w2_words[0, 0].bitcast(I32))
-        nc.sync.dma_start(out=gates[:], in_=gate[0:P, :])
-        load_words(w2w_rest, w2_words[1:E, 0])
-        load_scale_rows(w1s[1], w1_scales[2:E].rearrange("e s q i -> (e s) q i"))
-        for e in range(2, E):
+        load_words(w2w[0], w2_words[0])
+        for e in range(1, E):
+            load_scale_rows(w1s[e], w1_scales[e])
             load_words(w1w_rest[e - 1], w1_words[e])
+            if e == 1:
+                nc.sync.dma_start(out=gates[:], in_=gate[0:P, :])
+            elif e == 2:
+                load_words(w2w[1], w2_words[1])
+            else:
+                load_words(w2w_late, w2_words[2:E, 0])
 
         grouped = {}
 
         def cast(s):
             for a, b, eng in CASTS[s]:
-                tag = f"scales{s - 1}" if eng == "v" and s > 0 else f"grouped{s}_{a}"
+                tag = CAST_AFTER[s] if eng == "v" and s > 0 else f"grouped{s}_{a}"
                 grouped[s, a, b] = keep.tile([P, (b - a) * PACK], BF16, name=f"grouped{s}_{a}", tag=tag, align_bytes=64)
                 dst = grouped[s, a, b][:].rearrange("p (c i t) -> p c t i", i=4, t=PACK)
                 src = raw[s][:, :, a:b].rearrange("p t (c i) -> p c t i", i=4)
@@ -125,7 +135,7 @@ def tile_moe_pln_mlp_relu_kernel(
                 a0, b0 = [(c, d) for c, d, eng in CASTS[s] if c <= a and b <= d][0]
                 nc.vector.quantize_mx(
                     out=words[s][:, a:b].bitcast(FP8X4),
-                    scales=scales[s][:, a:b],
+                    scales=scales[0][4:P, a:b] if s == 1 else scales[s][:, a:b],
                     in_=grouped[s, a0, b0][:, (a - a0) * PACK : (b - a0) * PACK],
                 )
 
@@ -142,35 +152,38 @@ def tile_moe_pln_mlp_relu_kernel(
             dst = keep.tile([P, (e1 - e0) * C], U32, name=name, tag=tag or name, align_bytes=64)
             gather(slot_words, s, e0, e1, dst[:])
 
-        def gather_scales(s, e0, e1):
-            dst = keep.tile([P, (e1 - e0) * C], U8, name=f"slot_scales{s}_{e0}", align_bytes=64)
+        def gather_scales(s, e0, e1, tag=None):
+            name = f"slot_scales{s}_{e0}"
+            dst = keep.tile([P, (e1 - e0) * C], U8, name=name, tag=tag or name, align_bytes=64)
             gather(slot_scales, s, e0, e1, dst[:])
+            return dst
 
         acc = {}
 
         def layer1(e, s):
-            if s == 0:
-                acc[e] = psum.tile([P, H], F32, name=f"a{e}", tag=f"a{e}" if e < 2 else f"y{e - 2}_1")
+            if e not in acc:
+                acc[e] = psum.tile([P, H], F32, name=f"a{e}", tag=f"a{e}" if e < 2 else f"y{e - 2}_0")
             nc.tensor.matmul_mx(
                 out=acc[e][:],
                 lhsT=slot_words[s, e].bitcast(FP8X4),
                 lhsT_scale=slot_scales[s, e],
                 rhs=(w1w_first[s // 2][:, s % 2, :] if e == 0 else w1w_rest[e - 1][:, s, :]).bitcast(FP4X4),
-                rhs_scale=w1s[e // 2][:, (e % 2) * PASSES + s, :],
-                start=(s == 0),
-                stop=(s == (2 if e == 1 else 3)),
+                rhs_scale=w1s[e][:, s, :],
+                start=(s == PASS_ORDER[e][0]),
+                stop=(s == PASS_ORDER[e][-1]),
             )
 
-        h_homes, h_words, h_scales, y_rows = {}, {}, {}, {}
+        h_homes, h_words, h_scales, y_sums, y_rows = {}, {}, {}, {}, {}
 
         def hidden(e):
             h_rows = keep.tile([P, H], BF16, name=f"h_rows{e}", align_bytes=64)
-            nc.scalar.activation(
-                out=h_rows[:].rearrange("p (u m v) -> p u m v", u=2, v=2),
-                in_=acc[e][:].rearrange("p (m u v) -> p u m v", u=2, v=2),
-                func=RELU,
-            )
-            turned = psum.tile([P, 2, C], F32, name=f"turned{e}", tag="t" if e == 0 else Y_BANKS[e - 1][0])
+            for u in range(2):
+                nc.scalar.activation(
+                    out=h_rows[:].rearrange("p (u m v) -> p u m v", u=2, v=2)[:, u],
+                    in_=acc[e][:].rearrange("p (m u v) -> p u m v", u=2, v=2)[:, u],
+                    func=RELU,
+                )
+            turned = psum.tile([P, 2, C], F32, name=f"turned{e}", tag=f"t{e % 2}")
             pairs = h_rows[:].bitcast(F32)
             for u in range(2):
                 nc.tensor.transpose(turned[:, u, :], pairs[:, u * P : (u + 1) * P], ident[:])
@@ -186,22 +199,27 @@ def tile_moe_pln_mlp_relu_kernel(
                 )
 
         def hidden_quantize(e):
-            h_words[e] = keep.tile([P, C], U32, name=f"h_words{e}", align_bytes=64)
+            h_words[e] = keep.tile(
+                [P, C], U32, name=f"h_words{e}", tag="slot_words3_1" if e == 0 else f"h_words{e}", align_bytes=64
+            )
             h_scales[e] = keep.tile([P, C], U8, name=f"h_scales{e}", align_bytes=64)
             for a, b, home in h_homes[e]:
                 nc.vector.quantize_mx(
                     out=h_words[e][:, a:b].bitcast(FP8X4), scales=h_scales[e][:, a:b], in_=home.bitcast(BF16)
                 )
 
+        def block(e, i):
+            return (i + 2 * e) % BLOCKS
+
         def layer2(e):
-            w2 = w2w_first[:] if e == 0 else w2w_rest[:, e - 1, :]
-            y_rows[e] = keep.tile([P, BLOCKS * C], F32, name=f"y_rows{e}")
-            first = 2 * (e % 2)
-            for half, b0 in enumerate((first, 2 - first)):
-                y = psum.tile([P, 2 * C], F32, name=f"y{e}_{half}", tag=Y_BANKS[e][half])
-                for b in (b0, b0 + 1):
+            w2 = w2w[e][:, 0, :] if e < 2 else w2w_late[:, e - 2, :]
+            for part, (i0, i1) in enumerate(((0, 2), (2, BLOCKS))):
+                y = psum.tile([P, (i1 - i0) * C], F32, name=f"y{e}_{part}", tag=Y_BANKS[e][part])
+                y_sums[e, part] = y
+                for i in range(i0, i1):
+                    b = block(e, i)
                     nc.tensor.matmul_mx(
-                        out=y[:, (b - b0) * C : (b - b0 + 1) * C],
+                        out=y[:, (i - i0) * C : (i - i0 + 1) * C],
                         lhsT=w2[:, b * 2 * P : (b + 1) * 2 * P].bitcast(FP4X4),
                         lhsT_scale=w2s[:, e, b * P : (b + 1) * P],
                         rhs=h_words[e][:].bitcast(FP8X4),
@@ -209,12 +227,18 @@ def tile_moe_pln_mlp_relu_kernel(
                         start=True,
                         stop=True,
                     )
-                nc.scalar.activation(out=y_rows[e][:, b0 * C : (b0 + 2) * C], in_=y[:], func=COPY)
 
-        def scatter(e, b):
+        def leave(e, part):
+            name = f"y_rows{e}_{part}"
+            tag = f"h_rows{e + 1}" if part == 1 and e + 1 < E else name
+            y_rows[e, part] = keep.tile([P, 2 * C], F32, name=name, tag=tag, align_bytes=64)
+            nc.scalar.activation(out=y_rows[e, part][:], in_=y_sums[e, part][:], func=COPY)
+
+        def scatter(e, i):
+            b = block(e, i)
             nc.vector.tensor_tensor(
                 outs[b][:].indirect(offsets[:, e * OC : (e + 1) * OC]),
-                y_rows[e][:, b * C : (b + 1) * C],
+                y_rows[e, i // 2][:, (i % 2) * C : (i % 2 + 1) * C],
                 gates[:, e * C : (e + 1) * C],
                 MULT,
             )
@@ -224,42 +248,47 @@ def tile_moe_pln_mlp_relu_kernel(
         cast(0)
         quantize(0)
         gather_words(0, 0, E)
-        gather_scales(0, 0, E)
         cast(1)
         quantize(1)
-        gather_words(1, 0, 2)
-        gather_scales(1, 0, E)
+        both = gather_scales(0, 0, E)
+        nc.gpsimd.dma_start(out=shifted[0:100, :].bitcast(I32), in_=both[4:104, :].bitcast(I32))
+        for e in range(E):
+            slot_scales[1, e] = shifted[:, e * C : (e + 1) * C]
+        gather_words(1, 0, E)
         cast(2)
         quantize(2)
         gather_words(2, 0, 1)
-        gather_scales(2, 0, E)
+        gather_scales(2, 0, 1)
         cast(3)
         quantize(3)
         for e0, e1 in ((0, 1), (1, 2), (2, E)):
             gather_words(3, e0, e1)
             gather_scales(3, e0, e1)
+        gather_scales(2, 1, E, tag="scales3")
         for s in range(PASSES):
             layer1(0, s)
         hidden(0)
-        gather_words(2, 1, 2, tag="h_rows0")
-        for s in (0, 1, 3, 2):
+        for s in PASS_ORDER[1][:-1]:
             layer1(1, s)
         hidden_quantize(0)
-        late = keep.tile([P, 4 * C], U32, name="late_words", tag="h_first", align_bytes=64)
-        gather(slot_words, 1, 2, E, late[:, 0 : 2 * C])
-        gather(slot_words, 2, 2, E, late[:, 2 * C : 4 * C])
         layer2(0)
+        leave(0, 0)
+        late = keep.tile([P, (E - 1) * C], U32, name="late_words", tag="h_first", align_bytes=64)
+        gather(slot_words, 2, 1, 2, late[:, 0:C])
+        gather(slot_words, 2, 2, E, late[:, C:])
+        layer1(1, PASS_ORDER[1][-1])
         for e in range(E):
-            first = 2 * (e % 2)
             if e + 1 < E:
                 hidden(e + 1)
-            scatter(e, first)
-            scatter(e, first + 1)
+            leave(e, 1)
+            scatter(e, 0)
+            scatter(e, 1)
             if e + 2 < E:
                 for s in range(PASSES):
                     layer1(e + 2, s)
             if e + 1 < E:
                 hidden_quantize(e + 1)
                 layer2(e + 1)
-            scatter(e, 2 - first)
-            scatter(e, 3 - first)
+                leave(e + 1, 0)
+            scatter(e, 2)
+            scatter(e, 3)

@@ -14,7 +14,6 @@ PASSES = K // K_PASS
 W = 704
 OC = C // 16
 BLOCKS = N // P
-SPARE = C
 
 F32 = mybir.dt.float32
 BF16 = mybir.dt.bfloat16
@@ -29,19 +28,17 @@ RELU = mybir.ActivationFunctionType.Relu
 MULT = mybir.AluOpType.mult
 
 CASTS = {
-    0: ((0, 384, "v"), (384, 512, "v"), (512, 640, "s")),
+    0: ((0, 384, "v"), (384, 640, "s")),
     1: ((0, 256, "s"), (256, 384, "s"), (384, 640, "v")),
-    2: ((0, 512, "s"), (512, 640, "v")),
+    2: ((0, 512, "s"), (512, 640, "s")),
     3: ((0, 256, "v"), (256, 512, "s"), (512, 640, "s")),
 }
-Y_BANKS = (("y0_0", "y0_1"), ("y1_0", "y1_1"), ("a0", "a1"), ("t0", "y0_1"))
-PASS_ORDER = ((0, 1, 2, 3), (3, 0, 1, 2), (0, 1, 2, 3), (0, 1, 2, 3))
-CAST_AFTER = (None, "words0", "words1", "grouped2_0")
-CHUNKS = (((0, 384), (384, T)), ((0, T),), ((0, T),), ((0, T),))
+Y_BANKS = (("y0_0", "a1"), ("y1_0", "y1_1"), ("a0", "a1"), ("t0", "y3_1"))
+CAST_AFTER = (None, "words0", None, "grouped2_512")
 QUANTS = {
-    0: ((0, 256), (256, 384), (384, 512), (512, 640)),
+    0: ((0, 256), (256, 384), (384, 640)),
     1: ((0, 256), (384, 640), (256, 384)),
-    2: ((512, 640), (0, 512)),
+    2: ((0, 512), (512, 640)),
     3: ((0, 256), (256, 512), (512, 640)),
 }
 
@@ -60,14 +57,16 @@ def tile_moe_pln_mlp_relu_kernel(
         words = [keep.tile([P, W], I32, name=f"words{s}", align_bytes=64) for s in range(PASSES)]
         scales = {s: keep.tile([P, W], U8, name=f"scales{s}", align_bytes=64) for s in (0, 2, 3)}
         shifted = keep.tile([P, SLOTS], U8, name="shifted", align_bytes=64)
-        w1w_first = [keep.tile([P, 2, 2 * H], U8, name=f"w1w_first{u}", align_bytes=64) for u in range(2)]
-        w1w_rest = [keep.tile([P, PASSES, 2 * H], U8, name=f"w1w_rest{e}", align_bytes=64) for e in range(1, E)]
+        w1w_early = [
+            [keep.tile([P, 2, 2 * H], U8, name=f"w1w{e}_{u}", align_bytes=64) for u in range(2)] for e in range(2)
+        ]
+        w1w_late = [keep.tile([P, PASSES, 2 * H], U8, name=f"w1w{e}", align_bytes=64) for e in range(2, E)]
         w1s = [keep.tile([P, PASSES, H], U8, name=f"w1s{e}", align_bytes=64) for e in range(E)]
         w2w = [keep.tile([P, 1, 2 * N], U8, name=f"w2w{e}", align_bytes=64) for e in range(2)]
         w2w_late = keep.tile([P, 2, 2 * N], U8, name="w2w_late", align_bytes=64)
         w2s = keep.tile([P, E, N], U8, name="w2s", align_bytes=64)
         gates = keep.tile([P, SLOTS], F32, name="gates")
-        outs = [keep.tile([P, T + SPARE], F32, name=f"outs{b}", align_bytes=64) for b in range(BLOCKS)]
+        outs = [keep.tile([P, T], F32, name=f"outs{b}") for b in range(BLOCKS)]
         ident = keep.tile([P, P], F32, name="ident")
         zero = keep.tile([P, 1], F32, name="zero")
 
@@ -80,42 +79,40 @@ def tile_moe_pln_mlp_relu_kernel(
         for eng, tile in ((nc.gpsimd, w1s[0]), (nc.vector, w2s), (nc.gpsimd, w1s[1]), (nc.gpsimd, w1s[2]), (nc.gpsimd, w1s[3])):
             eng.memset(tile[:].rearrange("p s i -> p (s i)").bitcast(I32), 0)
         for s in range(PASSES):
-            if s == PASSES - 1:
-                load_scale_rows(w1s[0], w1_scales[0])
-            for a, b in CHUNKS[s]:
-                nc.sync.dma_start(
-                    out=raw[s][:, :, a:b],
-                    in_=xT[s * K_PASS : (s + 1) * K_PASS, a:b].rearrange("(p j) t -> p j t", j=PACK),
-                )
+            nc.sync.dma_start(
+                out=raw[s][:], in_=xT[s * K_PASS : (s + 1) * K_PASS, :].rearrange("(p j) t -> p j t", j=PACK)
+            )
             if s == 0:
                 nc.sync.dma_start(offsets[:], offs)
 
         nc.vector.memset(zero[:], 0.0)
         for b in range(1, BLOCKS):
-            nc.scalar.activation(out=outs[b][:, 0:T], in_=zero[:].to_broadcast([P, T]), func=COPY)
+            nc.scalar.activation(out=outs[b][:], in_=zero[:].to_broadcast([P, T]), func=COPY)
         make_identity(nc, ident[:])
         for s in range(PASSES):
             nc.vector.memset(words[s][:, T:W], 0)
         for tile in (scales[0], scales[2], scales[3], shifted):
             nc.vector.memset(tile[:].bitcast(I32), 0)
-        nc.vector.memset(outs[0][:, 0:T], 0.0)
+        nc.vector.memset(outs[0][:], 0.0)
 
         def load_words(tile, rows):
             nc.sync.dma_start(out=tile[:].bitcast(I32), in_=rows.rearrange("g p c -> p g c").bitcast(I32))
 
-        for u in range(2):
-            load_words(w1w_first[u], w1_words[0, 2 * u : 2 * u + 2])
+        load_scale_rows(w1s[0], w1_scales[0])
+        load_words(w1w_early[0][0], w1_words[0, 0:2])
+        load_words(w1w_early[0][1], w1_words[0, 2:4])
+        load_scale_rows(w1s[1], w1_scales[1])
+        load_words(w1w_early[1][0], w1_words[1, 0:2])
         load_scale_rows(w2s, w2_scales[:, 0])
         load_words(w2w[0], w2_words[0])
-        for e in range(1, E):
-            load_scale_rows(w1s[e], w1_scales[e])
-            load_words(w1w_rest[e - 1], w1_words[e])
-            if e == 1:
-                nc.sync.dma_start(out=gates[:], in_=gate[0:P, :])
-            elif e == 2:
-                load_words(w2w[1], w2_words[1])
-            else:
-                load_words(w2w_late, w2_words[2:E, 0])
+        load_words(w1w_early[1][1], w1_words[1, 2:4])
+        nc.sync.dma_start(out=gates[:], in_=gate[0:P, :])
+        load_scale_rows(w1s[2], w1_scales[2])
+        load_words(w1w_late[0], w1_words[2])
+        load_words(w2w[1], w2_words[1])
+        load_scale_rows(w1s[3], w1_scales[3])
+        load_words(w1w_late[1], w1_words[3])
+        load_words(w2w_late, w2_words[2:E, 0])
 
         grouped = {}
 
@@ -161,19 +158,19 @@ def tile_moe_pln_mlp_relu_kernel(
         acc = {}
 
         def layer1(e, s):
-            if e not in acc:
+            if s == 0:
                 acc[e] = psum.tile([P, H], F32, name=f"a{e}", tag=f"a{e}" if e < 2 else f"y{e - 2}_0")
             nc.tensor.matmul_mx(
                 out=acc[e][:],
                 lhsT=slot_words[s, e].bitcast(FP8X4),
                 lhsT_scale=slot_scales[s, e],
-                rhs=(w1w_first[s // 2][:, s % 2, :] if e == 0 else w1w_rest[e - 1][:, s, :]).bitcast(FP4X4),
+                rhs=(w1w_early[e][s // 2][:, s % 2, :] if e < 2 else w1w_late[e - 2][:, s, :]).bitcast(FP4X4),
                 rhs_scale=w1s[e][:, s, :],
-                start=(s == PASS_ORDER[e][0]),
-                stop=(s == PASS_ORDER[e][-1]),
+                start=(s == 0),
+                stop=(s == PASSES - 1),
             )
 
-        h_homes, h_words, h_scales, y_sums, y_rows = {}, {}, {}, {}, {}
+        h_grouped, h_words, h_scales, y_sums, y_rows = {}, {}, {}, {}, {}
 
         def hidden(e):
             h_rows = keep.tile([P, H], BF16, name=f"h_rows{e}", align_bytes=64)
@@ -187,46 +184,32 @@ def tile_moe_pln_mlp_relu_kernel(
             pairs = h_rows[:].bitcast(F32)
             for u in range(2):
                 nc.tensor.transpose(turned[:, u, :], pairs[:, u * P : (u + 1) * P], ident[:])
-            if e == 0:
-                first = keep.tile([P, 2 * C], F32, name="h_first", tag="h_first", align_bytes=64)
-                h_homes[e] = [(0, C, first[:])]
-            else:
-                b0 = 2 * (e % 2)
-                h_homes[e] = [(0, C // 2, outs[b0][:, T:]), (C // 2, C, outs[b0 + 1][:, T:])]
-            for a, b, home in h_homes[e]:
-                nc.scalar.copy(
-                    out=home.rearrange("p (c u) -> p c u", u=2), in_=turned[:, :, a:b].rearrange("p u c -> p c u")
-                )
+            h_grouped[e] = keep.tile([P, 2 * C], F32, name=f"h_grouped{e}", align_bytes=64)
+            nc.scalar.copy(
+                out=h_grouped[e][:].rearrange("p (c u) -> p c u", u=2), in_=turned[:].rearrange("p u c -> p c u")
+            )
 
         def hidden_quantize(e):
-            h_words[e] = keep.tile(
-                [P, C], U32, name=f"h_words{e}", tag="slot_words3_1" if e == 0 else f"h_words{e}", align_bytes=64
-            )
+            h_words[e] = keep.tile([P, C], U32, name=f"h_words{e}", align_bytes=64)
             h_scales[e] = keep.tile([P, C], U8, name=f"h_scales{e}", align_bytes=64)
-            for a, b, home in h_homes[e]:
-                nc.vector.quantize_mx(
-                    out=h_words[e][:, a:b].bitcast(FP8X4), scales=h_scales[e][:, a:b], in_=home.bitcast(BF16)
-                )
+            nc.vector.quantize_mx(
+                out=h_words[e][:].bitcast(FP8X4), scales=h_scales[e][:], in_=h_grouped[e][:].bitcast(BF16)
+            )
 
-        def block(e, i):
-            return (i + 2 * e) % BLOCKS
-
-        def layer2(e):
+        def layer2(e, part):
             w2 = w2w[e][:, 0, :] if e < 2 else w2w_late[:, e - 2, :]
-            for part, (i0, i1) in enumerate(((0, 2), (2, BLOCKS))):
-                y = psum.tile([P, (i1 - i0) * C], F32, name=f"y{e}_{part}", tag=Y_BANKS[e][part])
-                y_sums[e, part] = y
-                for i in range(i0, i1):
-                    b = block(e, i)
-                    nc.tensor.matmul_mx(
-                        out=y[:, (i - i0) * C : (i - i0 + 1) * C],
-                        lhsT=w2[:, b * 2 * P : (b + 1) * 2 * P].bitcast(FP4X4),
-                        lhsT_scale=w2s[:, e, b * P : (b + 1) * P],
-                        rhs=h_words[e][:].bitcast(FP8X4),
-                        rhs_scale=h_scales[e][:],
-                        start=True,
-                        stop=True,
-                    )
+            y_sums[e, part] = psum.tile([P, 2 * C], F32, name=f"y{e}_{part}", tag=Y_BANKS[e][part])
+            for i in range(2):
+                b = 2 * part + i
+                nc.tensor.matmul_mx(
+                    out=y_sums[e, part][:, i * C : (i + 1) * C],
+                    lhsT=w2[:, b * 2 * P : (b + 1) * 2 * P].bitcast(FP4X4),
+                    lhsT_scale=w2s[:, e, b * P : (b + 1) * P],
+                    rhs=h_words[e][:].bitcast(FP8X4),
+                    rhs_scale=h_scales[e][:],
+                    start=True,
+                    stop=True,
+                )
 
         def leave(e, part):
             name = f"y_rows{e}_{part}"
@@ -234,16 +217,15 @@ def tile_moe_pln_mlp_relu_kernel(
             y_rows[e, part] = keep.tile([P, 2 * C], F32, name=name, tag=tag, align_bytes=64)
             nc.scalar.activation(out=y_rows[e, part][:], in_=y_sums[e, part][:], func=COPY)
 
-        def scatter(e, i):
-            b = block(e, i)
+        def scatter(e, b):
             nc.vector.tensor_tensor(
                 outs[b][:].indirect(offsets[:, e * OC : (e + 1) * OC]),
-                y_rows[e, i // 2][:, (i % 2) * C : (i % 2 + 1) * C],
+                y_rows[e, b // 2][:, (b % 2) * C : (b % 2 + 1) * C],
                 gates[:, e * C : (e + 1) * C],
                 MULT,
             )
             if e == E - 1:
-                nc.sync.dma_start(out=out[b * P : (b + 1) * P, :], in_=outs[b][:, 0:T])
+                nc.sync.dma_start(out=out[b * P : (b + 1) * P, :], in_=outs[b][:])
 
         cast(0)
         quantize(0)
@@ -261,25 +243,30 @@ def tile_moe_pln_mlp_relu_kernel(
         gather_scales(2, 0, 1)
         cast(3)
         quantize(3)
-        for e0, e1 in ((0, 1), (1, 2), (2, E)):
-            gather_words(3, e0, e1)
-            gather_scales(3, e0, e1)
-        gather_scales(2, 1, E, tag="scales3")
+        for e in range(2):
+            gather_words(3, e, e + 1)
+            gather_scales(3, e, e + 1)
+        gather_scales(3, 2, E)
         for s in range(PASSES):
             layer1(0, s)
+        gather_words(2, 1, 2, tag="slot_scales3_0")
+        gather_scales(2, 1, E, tag="scales3")
         hidden(0)
-        for s in PASS_ORDER[1][:-1]:
-            layer1(1, s)
+        layer1(1, 0)
+        layer1(1, 1)
         hidden_quantize(0)
-        layer2(0)
+        layer2(0, 0)
         leave(0, 0)
-        late = keep.tile([P, (E - 1) * C], U32, name="late_words", tag="h_first", align_bytes=64)
-        gather(slot_words, 2, 1, 2, late[:, 0:C])
-        gather(slot_words, 2, 2, E, late[:, C:])
-        layer1(1, PASS_ORDER[1][-1])
+        layer1(1, 2)
+        layer1(1, 3)
+        late = keep.tile([P, 4 * C], U32, name="late_words", tag="h_grouped0", align_bytes=64)
+        gather(slot_words, 2, 2, E, late[:, 0 : 2 * C])
+        gather(slot_words, 3, 2, E, late[:, 2 * C :])
         for e in range(E):
             if e + 1 < E:
                 hidden(e + 1)
+            if e == 0:
+                layer2(0, 1)
             leave(e, 1)
             scatter(e, 0)
             scatter(e, 1)
@@ -288,7 +275,8 @@ def tile_moe_pln_mlp_relu_kernel(
                     layer1(e + 2, s)
             if e + 1 < E:
                 hidden_quantize(e + 1)
-                layer2(e + 1)
+                layer2(e + 1, 0)
                 leave(e + 1, 0)
+                layer2(e + 1, 1)
             scatter(e, 2)
             scatter(e, 3)

@@ -57,10 +57,7 @@ def tile_moe_pln_mlp_relu_kernel(
         words = [keep.tile([P, W], I32, name=f"words{s}", align_bytes=64) for s in range(PASSES)]
         scales = {s: keep.tile([P, W], U8, name=f"scales{s}", align_bytes=64) for s in (0, 2, 3)}
         shifted = keep.tile([P, SLOTS], U8, name="shifted", align_bytes=64)
-        w1w_early = [
-            [keep.tile([P, 2, 2 * H], U8, name=f"w1w{e}_{u}", align_bytes=64) for u in range(2)] for e in range(2)
-        ]
-        w1w_late = [keep.tile([P, PASSES, 2 * H], U8, name=f"w1w{e}", align_bytes=64) for e in range(2, E)]
+        w1w = {}
         w1s = [keep.tile([P, PASSES, H], U8, name=f"w1s{e}", align_bytes=64) for e in range(E)]
         w2w = [keep.tile([P, 1, 2 * N], U8, name=f"w2w{e}", align_bytes=64) for e in range(2)]
         w2w_late = keep.tile([P, 2, 2 * N], U8, name="w2w_late", align_bytes=64)
@@ -98,21 +95,11 @@ def tile_moe_pln_mlp_relu_kernel(
         def load_words(tile, rows):
             nc.sync.dma_start(out=tile[:].bitcast(I32), in_=rows.rearrange("g p c -> p g c").bitcast(I32))
 
-        load_scale_rows(w1s[0], w1_scales[0])
-        load_words(w1w_early[0][0], w1_words[0, 0:2])
-        load_words(w1w_early[0][1], w1_words[0, 2:4])
-        load_scale_rows(w1s[1], w1_scales[1])
-        load_words(w1w_early[1][0], w1_words[1, 0:2])
-        load_scale_rows(w2s, w2_scales[:, 0])
-        load_words(w2w[0], w2_words[0])
-        load_words(w1w_early[1][1], w1_words[1, 2:4])
-        nc.sync.dma_start(out=gates[:], in_=gate[0:P, :])
-        load_scale_rows(w1s[2], w1_scales[2])
-        load_words(w1w_late[0], w1_words[2])
-        load_words(w2w[1], w2_words[1])
-        load_scale_rows(w1s[3], w1_scales[3])
-        load_words(w1w_late[1], w1_words[3])
-        load_words(w2w_late, w2_words[2:E, 0])
+        def load_first(e, s0, s1):
+            tile = keep.tile([P, s1 - s0, 2 * H], U8, name=f"w1w{e}_{s0}", align_bytes=64)
+            load_words(tile, w1_words[e, s0:s1])
+            for s in range(s0, s1):
+                w1w[e, s] = tile[:, s - s0, :]
 
         grouped = {}
 
@@ -164,7 +151,7 @@ def tile_moe_pln_mlp_relu_kernel(
                 out=acc[e][:],
                 lhsT=slot_words[s, e].bitcast(FP8X4),
                 lhsT_scale=slot_scales[s, e],
-                rhs=(w1w_early[e][s // 2][:, s % 2, :] if e < 2 else w1w_late[e - 2][:, s, :]).bitcast(FP4X4),
+                rhs=w1w[e, s].bitcast(FP4X4),
                 rhs_scale=w1s[e][:, s, :],
                 start=(s == 0),
                 stop=(s == PASSES - 1),
@@ -233,7 +220,23 @@ def tile_moe_pln_mlp_relu_kernel(
         cast(1)
         quantize(1)
         both = gather_scales(0, 0, E)
-        nc.gpsimd.dma_start(out=shifted[0:100, :].bitcast(I32), in_=both[4:104, :].bitcast(I32))
+        load_scale_rows(w1s[0], w1_scales[0])
+        load_first(0, 0, 2)
+        nc.sync.dma_start(out=shifted[0:100, :].bitcast(I32), in_=both[4:104, :].bitcast(I32))
+        load_first(0, 2, 4)
+        load_scale_rows(w1s[1], w1_scales[1])
+        load_first(1, 0, 3)
+        load_scale_rows(w2s, w2_scales[:, 0])
+        load_words(w2w[0], w2_words[0])
+        load_first(1, 3, 4)
+        nc.sync.dma_start(out=gates[:], in_=gate[0:P, :])
+        load_scale_rows(w1s[2], w1_scales[2])
+        load_first(2, 0, 4)
+        load_words(w2w[1], w2_words[1])
+        load_scale_rows(w1s[3], w1_scales[3])
+        load_first(3, 0, 4)
+        load_words(w2w_late, w2_words[2:E, 0])
+
         for e in range(E):
             slot_scales[1, e] = shifted[:, e * C : (e + 1) * C]
         gather_words(1, 0, E)
@@ -250,15 +253,15 @@ def tile_moe_pln_mlp_relu_kernel(
         for s in range(PASSES):
             layer1(0, s)
         gather_words(2, 1, 2, tag="slot_scales3_0")
-        gather_scales(2, 1, E, tag="scales3")
+        gather_scales(2, 1, 2, tag="slot_words3_0")
         hidden(0)
-        layer1(1, 0)
-        layer1(1, 1)
+        gather_scales(2, 2, E, tag="w1w0_2")
+        for s in range(PASSES - 1):
+            layer1(1, s)
         hidden_quantize(0)
         layer2(0, 0)
         leave(0, 0)
-        layer1(1, 2)
-        layer1(1, 3)
+        layer1(1, PASSES - 1)
         late = keep.tile([P, 4 * C], U32, name="late_words", tag="h_grouped0", align_bytes=64)
         gather(slot_words, 2, 2, E, late[:, 0 : 2 * C])
         gather(slot_words, 3, 2, E, late[:, 2 * C :])

@@ -11,9 +11,14 @@ P = 128
 PACK = 4
 K_PASS = P * PACK
 PASSES = K // K_PASS
-W = 704
-OC = C // 16
+LAST = PASSES - 1
+WINDOW = 704
+LIST_COLS = C // 16
 BLOCKS = N // P
+QUADRANT = 32
+PACKED_ROW = 4
+SCALE_SPAN = 3 * QUADRANT + 4
+RUN = 4
 
 F32 = mybir.dt.float32
 BF16 = mybir.dt.bfloat16
@@ -27,20 +32,21 @@ COPY = mybir.ActivationFunctionType.Copy
 RELU = mybir.ActivationFunctionType.Relu
 MULT = mybir.AluOpType.mult
 
-CASTS = {
-    0: ((0, 384, "v"), (384, 640, "s")),
-    1: ((0, 256, "s"), (256, 384, "s"), (384, 640, "v")),
-    2: ((0, 512, "s"), (512, 640, "s")),
-    3: ((0, 256, "v"), (256, 512, "s"), (512, 640, "s")),
-}
+CASTS = (
+    ((0, 384, "vector"), (384, 640, "scalar")),
+    ((0, 256, "scalar"), (256, 384, "scalar"), (384, 640, "vector")),
+    ((0, 512, "scalar"), (512, 640, "scalar")),
+    ((0, 128, "vector"), (128, 384, "scalar"), (384, 512, "scalar"), (512, 640, "scalar")),
+)
+VECTOR_CAST_TAG = {1: "words0", LAST: "grouped2_512"}
+QUANTS = (
+    ((0, 256), (256, 384), (384, 640)),
+    ((0, 256), (384, 640), (256, 384)),
+    ((0, 512), (512, 640)),
+    ((0, 128), (128, 384), (384, 512), (512, 640)),
+)
 Y_BANKS = (("y0_0", "a1"), ("y1_0", "y1_1"), ("a0", "a1"), ("t0", "y3_1"))
-CAST_AFTER = (None, "words0", None, "grouped2_512")
-QUANTS = {
-    0: ((0, 256), (256, 384), (384, 640)),
-    1: ((0, 256), (384, 640), (256, 384)),
-    2: ((0, 512), (512, 640)),
-    3: ((0, 256), (256, 512), (512, 640)),
-}
+A_BANKS = ("a0", "a1", "y0_0", "y1_0")
 
 
 def tile_moe_pln_mlp_relu_kernel(
@@ -54,10 +60,9 @@ def tile_moe_pln_mlp_relu_kernel(
         offsets = keep.tile([P, SLOTS // 16], U16, name="offsets")
 
         raw = [keep.tile([P, PACK, T], F32, name=f"raw{s}") for s in range(PASSES)]
-        words = [keep.tile([P, W], I32, name=f"words{s}", align_bytes=64) for s in range(PASSES)]
-        scales = {s: keep.tile([P, W], U8, name=f"scales{s}", align_bytes=64) for s in (0, 2, 3)}
+        words = [keep.tile([P, WINDOW], I32, name=f"words{s}", align_bytes=64) for s in range(PASSES)]
+        scales = {s: keep.tile([P, WINDOW], U8, name=f"scales{s}", align_bytes=64) for s in (0, 2, 3)}
         shifted = keep.tile([P, SLOTS], U8, name="shifted", align_bytes=64)
-        w1w = {}
         w1s = [keep.tile([P, PASSES, H], U8, name=f"w1s{e}", align_bytes=64) for e in range(E)]
         w2w = [keep.tile([P, 1, 2 * N], U8, name=f"w2w{e}", align_bytes=64) for e in range(2)]
         w2w_late = keep.tile([P, 2, 2 * N], U8, name="w2w_late", align_bytes=64)
@@ -67,14 +72,11 @@ def tile_moe_pln_mlp_relu_kernel(
         ident = keep.tile([P, P], F32, name="ident")
         zero = keep.tile([P, 1], F32, name="zero")
 
-        def load_scale_rows(tile, rows):
-            for r in range(4):
-                nc.sync.dma_start(
-                    out=tile[r:P:32, :, :].bitcast(I32), in_=rows[:, r:16:4, :].rearrange("g q i -> q g i").bitcast(I32)
-                )
+        nc.gpsimd.memset(w1s[0][:].rearrange("p s i -> p (s i)").bitcast(I32), 0)
+        nc.vector.memset(w2s[:].rearrange("p s i -> p (s i)").bitcast(I32), 0)
+        for e in range(1, E):
+            nc.gpsimd.memset(w1s[e][:].rearrange("p s i -> p (s i)").bitcast(I32), 0)
 
-        for eng, tile in ((nc.gpsimd, w1s[0]), (nc.vector, w2s), (nc.gpsimd, w1s[1]), (nc.gpsimd, w1s[2]), (nc.gpsimd, w1s[3])):
-            eng.memset(tile[:].rearrange("p s i -> p (s i)").bitcast(I32), 0)
         for s in range(PASSES):
             nc.sync.dma_start(
                 out=raw[s][:], in_=xT[s * K_PASS : (s + 1) * K_PASS, :].rearrange("(p j) t -> p j t", j=PACK)
@@ -87,15 +89,24 @@ def tile_moe_pln_mlp_relu_kernel(
             nc.scalar.activation(out=outs[b][:], in_=zero[:].to_broadcast([P, T]), func=COPY)
         make_identity(nc, ident[:])
         for s in range(PASSES):
-            nc.vector.memset(words[s][:, T:W], 0)
+            nc.vector.memset(words[s][:, T:WINDOW], 0)
         for tile in (scales[0], scales[2], scales[3], shifted):
             nc.vector.memset(tile[:].bitcast(I32), 0)
         nc.vector.memset(outs[0][:], 0.0)
 
+        def load_scale_rows(tile, rows):
+            for r in range(4):
+                nc.sync.dma_start(
+                    out=tile[r:P:QUADRANT, :, :].bitcast(I32),
+                    in_=rows[:, r:16:4, :].rearrange("g q i -> q g i").bitcast(I32),
+                )
+
         def load_words(tile, rows):
             nc.sync.dma_start(out=tile[:].bitcast(I32), in_=rows.rearrange("g p c -> p g c").bitcast(I32))
 
-        def load_first(e, s0, s1):
+        w1w = {}
+
+        def load_w1(e, s0, s1):
             tile = keep.tile([P, s1 - s0, 2 * H], U8, name=f"w1w{e}_{s0}", align_bytes=64)
             load_words(tile, w1_words[e, s0:s1])
             for s in range(s0, s1):
@@ -104,57 +115,57 @@ def tile_moe_pln_mlp_relu_kernel(
         grouped = {}
 
         def cast(s):
-            for a, b, eng in CASTS[s]:
-                tag = CAST_AFTER[s] if eng == "v" and s > 0 else f"grouped{s}_{a}"
-                grouped[s, a, b] = keep.tile([P, (b - a) * PACK], BF16, name=f"grouped{s}_{a}", tag=tag, align_bytes=64)
-                dst = grouped[s, a, b][:].rearrange("p (c i t) -> p c t i", i=4, t=PACK)
-                src = raw[s][:, :, a:b].rearrange("p t (c i) -> p c t i", i=4)
-                if eng == "v":
+            for t0, t1, engine in CASTS[s]:
+                name = f"grouped{s}_{t0}"
+                tag = VECTOR_CAST_TAG.get(s, name) if engine == "vector" else name
+                grouped[s, t0, t1] = keep.tile([P, (t1 - t0) * PACK], BF16, name=name, tag=tag, align_bytes=64)
+                dst = grouped[s, t0, t1][:].rearrange("p (c i t) -> p c t i", i=RUN, t=PACK)
+                src = raw[s][:, :, t0:t1].rearrange("p t (c i) -> p c t i", i=RUN)
+                if engine == "vector":
                     nc.vector.tensor_copy(out=dst, in_=src)
                 else:
                     nc.scalar.activation(out=dst, in_=src, func=COPY)
 
         def quantize(s):
-            for a, b in QUANTS[s]:
-                a0, b0 = [(c, d) for c, d, eng in CASTS[s] if c <= a and b <= d][0]
+            for t0, t1 in QUANTS[s]:
+                c0, c1 = [(a, b) for a, b, engine in CASTS[s] if a <= t0 and t1 <= b][0]
                 nc.vector.quantize_mx(
-                    out=words[s][:, a:b].bitcast(FP8X4),
-                    scales=scales[0][4:P, a:b] if s == 1 else scales[s][:, a:b],
-                    in_=grouped[s, a0, b0][:, (a - a0) * PACK : (b - a0) * PACK],
+                    out=words[s][:, t0:t1].bitcast(FP8X4),
+                    scales=scales[0][PACKED_ROW:P, t0:t1] if s == 1 else scales[s][:, t0:t1],
+                    in_=grouped[s, c0, c1][:, (t0 - c0) * PACK : (t1 - c0) * PACK],
                 )
 
         slot_words, slot_scales = {}, {}
 
-        def gather(kind, s, e0, e1, dst):
-            src = words[s][:].bitcast(U32) if kind is slot_words else scales[s][:]
-            nc.vector.tensor_copy(out=dst, in_=src.indirect(offsets[:, e0 * OC : e1 * OC]))
+        def gather(window, found, s, e0, e1, dst):
+            nc.vector.tensor_copy(out=dst, in_=window.indirect(offsets[:, e0 * LIST_COLS : e1 * LIST_COLS]))
             for e in range(e0, e1):
-                kind[s, e] = dst[:, (e - e0) * C : (e - e0 + 1) * C]
+                found[s, e] = dst[:, (e - e0) * C : (e - e0 + 1) * C]
 
         def gather_words(s, e0, e1, tag=None):
             name = f"slot_words{s}_{e0}"
             dst = keep.tile([P, (e1 - e0) * C], U32, name=name, tag=tag or name, align_bytes=64)
-            gather(slot_words, s, e0, e1, dst[:])
+            gather(words[s][:].bitcast(U32), slot_words, s, e0, e1, dst[:])
 
         def gather_scales(s, e0, e1, tag=None):
             name = f"slot_scales{s}_{e0}"
             dst = keep.tile([P, (e1 - e0) * C], U8, name=name, tag=tag or name, align_bytes=64)
-            gather(slot_scales, s, e0, e1, dst[:])
+            gather(scales[s][:], slot_scales, s, e0, e1, dst[:])
             return dst
 
-        acc = {}
+        a_sums = {}
 
         def layer1(e, s):
             if s == 0:
-                acc[e] = psum.tile([P, H], F32, name=f"a{e}", tag=f"a{e}" if e < 2 else f"y{e - 2}_0")
+                a_sums[e] = psum.tile([P, H], F32, name=f"a{e}", tag=A_BANKS[e])
             nc.tensor.matmul_mx(
-                out=acc[e][:],
+                out=a_sums[e][:],
                 lhsT=slot_words[s, e].bitcast(FP8X4),
                 lhsT_scale=slot_scales[s, e],
                 rhs=w1w[e, s].bitcast(FP4X4),
                 rhs_scale=w1s[e][:, s, :],
                 start=(s == 0),
-                stop=(s == PASSES - 1),
+                stop=(s == LAST),
             )
 
         h_grouped, h_words, h_scales, y_sums, y_rows = {}, {}, {}, {}, {}
@@ -164,7 +175,7 @@ def tile_moe_pln_mlp_relu_kernel(
             for u in range(2):
                 nc.scalar.activation(
                     out=h_rows[:].rearrange("p (u m v) -> p u m v", u=2, v=2)[:, u],
-                    in_=acc[e][:].rearrange("p (m u v) -> p u m v", u=2, v=2)[:, u],
+                    in_=a_sums[e][:].rearrange("p (m u v) -> p u m v", u=2, v=2)[:, u],
                     func=RELU,
                 )
             turned = psum.tile([P, 2, C], F32, name=f"turned{e}", tag=f"t{e % 2}")
@@ -183,13 +194,13 @@ def tile_moe_pln_mlp_relu_kernel(
                 out=h_words[e][:].bitcast(FP8X4), scales=h_scales[e][:], in_=h_grouped[e][:].bitcast(BF16)
             )
 
-        def layer2(e, part):
+        def layer2(e, half):
             w2 = w2w[e][:, 0, :] if e < 2 else w2w_late[:, e - 2, :]
-            y_sums[e, part] = psum.tile([P, 2 * C], F32, name=f"y{e}_{part}", tag=Y_BANKS[e][part])
+            y_sums[e, half] = psum.tile([P, 2 * C], F32, name=f"y{e}_{half}", tag=Y_BANKS[e][half])
             for i in range(2):
-                b = 2 * part + i
+                b = 2 * half + i
                 nc.tensor.matmul_mx(
-                    out=y_sums[e, part][:, i * C : (i + 1) * C],
+                    out=y_sums[e, half][:, i * C : (i + 1) * C],
                     lhsT=w2[:, b * 2 * P : (b + 1) * 2 * P].bitcast(FP4X4),
                     lhsT_scale=w2s[:, e, b * P : (b + 1) * P],
                     rhs=h_words[e][:].bitcast(FP8X4),
@@ -198,15 +209,15 @@ def tile_moe_pln_mlp_relu_kernel(
                     stop=True,
                 )
 
-        def leave(e, part):
-            name = f"y_rows{e}_{part}"
-            tag = f"h_rows{e + 1}" if part == 1 and e + 1 < E else name
-            y_rows[e, part] = keep.tile([P, 2 * C], F32, name=name, tag=tag, align_bytes=64)
-            nc.scalar.activation(out=y_rows[e, part][:], in_=y_sums[e, part][:], func=COPY)
+        def leave(e, half):
+            name = f"y_rows{e}_{half}"
+            tag = f"h_rows{e + 1}" if half == 1 and e + 1 < E else name
+            y_rows[e, half] = keep.tile([P, 2 * C], F32, name=name, tag=tag, align_bytes=64)
+            nc.scalar.activation(out=y_rows[e, half][:], in_=y_sums[e, half][:], func=COPY)
 
         def scatter(e, b):
             nc.vector.tensor_tensor(
-                outs[b][:].indirect(offsets[:, e * OC : (e + 1) * OC]),
+                outs[b][:].indirect(offsets[:, e * LIST_COLS : (e + 1) * LIST_COLS]),
                 y_rows[e, b // 2][:, (b % 2) * C : (b % 2 + 1) * C],
                 gates[:, e * C : (e + 1) * C],
                 MULT,
@@ -219,52 +230,59 @@ def tile_moe_pln_mlp_relu_kernel(
         gather_words(0, 0, E)
         cast(1)
         quantize(1)
-        both = gather_scales(0, 0, E)
+        packed = gather_scales(0, 0, E)
+
         load_scale_rows(w1s[0], w1_scales[0])
-        load_first(0, 0, 2)
-        nc.sync.dma_start(out=shifted[0:100, :].bitcast(I32), in_=both[4:104, :].bitcast(I32))
-        load_first(0, 2, 4)
+        load_w1(0, 0, 2)
+        nc.sync.dma_start(
+            out=shifted[0:SCALE_SPAN, :].bitcast(I32),
+            in_=packed[PACKED_ROW : PACKED_ROW + SCALE_SPAN, :].bitcast(I32),
+        )
+        load_w1(0, 2, PASSES)
         load_scale_rows(w1s[1], w1_scales[1])
-        load_first(1, 0, 3)
+        load_w1(1, 0, LAST)
         load_scale_rows(w2s, w2_scales[:, 0])
         load_words(w2w[0], w2_words[0])
-        load_first(1, 3, 4)
+        load_w1(1, LAST, PASSES)
         nc.sync.dma_start(out=gates[:], in_=gate[0:P, :])
         load_scale_rows(w1s[2], w1_scales[2])
-        load_first(2, 0, 4)
+        load_w1(2, 0, PASSES)
         load_words(w2w[1], w2_words[1])
         load_scale_rows(w1s[3], w1_scales[3])
-        load_first(3, 0, 4)
+        load_w1(3, 0, PASSES)
         load_words(w2w_late, w2_words[2:E, 0])
-
         for e in range(E):
             slot_scales[1, e] = shifted[:, e * C : (e + 1) * C]
         gather_words(1, 0, E)
+
         cast(2)
         quantize(2)
         gather_words(2, 0, 1)
         gather_scales(2, 0, 1)
-        cast(3)
-        quantize(3)
+        cast(LAST)
+        quantize(LAST)
         for e in range(2):
-            gather_words(3, e, e + 1)
-            gather_scales(3, e, e + 1)
-        gather_scales(3, 2, E)
+            gather_words(LAST, e, e + 1)
+            gather_scales(LAST, e, e + 1)
+        gather_scales(LAST, 2, E)
         for s in range(PASSES):
             layer1(0, s)
+
         gather_words(2, 1, 2, tag="slot_scales3_0")
         gather_scales(2, 1, 2, tag="slot_words3_0")
         hidden(0)
         gather_scales(2, 2, E, tag="w1w0_2")
-        for s in range(PASSES - 1):
+        for s in range(LAST):
             layer1(1, s)
         hidden_quantize(0)
         layer2(0, 0)
         leave(0, 0)
-        layer1(1, PASSES - 1)
+        layer1(1, LAST)
+
         late = keep.tile([P, 4 * C], U32, name="late_words", tag="h_grouped0", align_bytes=64)
-        gather(slot_words, 2, 2, E, late[:, 0 : 2 * C])
-        gather(slot_words, 3, 2, E, late[:, 2 * C :])
+        gather(words[2][:].bitcast(U32), slot_words, 2, 2, E, late[:, 0 : 2 * C])
+        gather(words[LAST][:].bitcast(U32), slot_words, LAST, 2, E, late[:, 2 * C :])
+
         for e in range(E):
             if e + 1 < E:
                 hidden(e + 1)

@@ -32,20 +32,18 @@ COPY = mybir.ActivationFunctionType.Copy
 RELU = mybir.ActivationFunctionType.Relu
 MULT = mybir.AluOpType.mult
 
-CASTS = (
-    ((0, 384, "vector"), (384, 640, "scalar")),
-    ((0, 256, "scalar"), (256, 384, "scalar"), (384, 640, "vector")),
-    ((0, 512, "scalar"), (512, 640, "scalar")),
-    ((0, 128, "vector"), (128, 384, "scalar"), (384, 512, "scalar"), (512, 640, "scalar")),
+PIECES = ((0, 256), (256, 512), (512, 640))
+SHARED = ((0, 256, "scalar", 0), (256, 384, "scalar", 256), (384, 512, "vector", 384), (512, 640, "vector", 512))
+SCALAR_ALONE = ((0, 256, "scalar", 0), (256, 512, "scalar", 256), (512, 640, "scalar", 512))
+LAST_ON_VECTOR = ((0, 256, "scalar", 0), (512, 640, "vector", 512), (256, 512, "scalar", 256))
+CASTS = (SHARED, SHARED, SCALAR_ALONE, SHARED)
+Y_UNITS = (
+    (((0,), "y0_0"), ((1,), "y3_1"), ((2, 3), "a1")),
+    (((0, 1), "y1_0"), ((2, 3), "y1_1")),
+    (((0, 1), "a0"), ((2, 3), "a1")),
+    (((0, 1), "t0"), ((2, 3), "y3_1")),
 )
-VECTOR_CAST_TAG = {1: "words0", LAST: "grouped2_512"}
-QUANTS = (
-    ((0, 256), (256, 384), (384, 640)),
-    ((0, 256), (384, 640), (256, 384)),
-    ((0, 512), (512, 640)),
-    ((0, 128), (128, 384), (384, 512), (512, 640)),
-)
-Y_BANKS = (("y0_0", "a1"), ("y1_0", "y1_1"), ("a0", "a1"), ("t0", "y3_1"))
+QUARTER_BANKS = (("a0", "y1_1", "y3_1", "t1"), ("a1", "y1_0", "a0", "y1_1"))
 A_BANKS = ("a0", "a1", "y0_0", "y1_0")
 
 
@@ -59,7 +57,9 @@ def tile_moe_pln_mlp_relu_kernel(
 
         offsets = keep.tile([P, SLOTS // 16], U16, name="offsets")
 
-        raw = [keep.tile([P, PACK, T], F32, name=f"raw{s}") for s in range(PASSES)]
+        raw = {
+            (s, t0): keep.tile([P, PACK, t1 - t0], F32, name=f"raw{s}_{t0}") for s in range(PASSES) for t0, t1 in PIECES
+        }
         words = [keep.tile([P, WINDOW], I32, name=f"words{s}", align_bytes=64) for s in range(PASSES)]
         scales = {s: keep.tile([P, WINDOW], U8, name=f"scales{s}", align_bytes=64) for s in (0, 2, 3)}
         shifted = keep.tile([P, SLOTS], U8, name="shifted", align_bytes=64)
@@ -72,26 +72,19 @@ def tile_moe_pln_mlp_relu_kernel(
         ident = keep.tile([P, P], F32, name="ident")
         zero = keep.tile([P, 1], F32, name="zero")
 
-        nc.gpsimd.memset(w1s[0][:].rearrange("p s i -> p (s i)").bitcast(I32), 0)
-        nc.vector.memset(w2s[:].rearrange("p s i -> p (s i)").bitcast(I32), 0)
-        for e in range(1, E):
-            nc.gpsimd.memset(w1s[e][:].rearrange("p s i -> p (s i)").bitcast(I32), 0)
-
-        for s in range(PASSES):
-            nc.sync.dma_start(
-                out=raw[s][:], in_=xT[s * K_PASS : (s + 1) * K_PASS, :].rearrange("(p j) t -> p j t", j=PACK)
-            )
-            if s == 0:
-                nc.sync.dma_start(offsets[:], offs)
-
         nc.vector.memset(zero[:], 0.0)
-        for b in range(1, BLOCKS):
+        for b in range(2, BLOCKS):
             nc.scalar.activation(out=outs[b][:], in_=zero[:].to_broadcast([P, T]), func=COPY)
+        for tile in w1s[1:]:
+            nc.gpsimd.memset(tile[:].rearrange("p s i -> p (s i)").bitcast(I32), 0)
         make_identity(nc, ident[:])
+        nc.gpsimd.memset(outs[1][:], 0.0)
         for s in range(PASSES):
             nc.vector.memset(words[s][:, T:WINDOW], 0)
         for tile in (scales[0], scales[2], scales[3], shifted):
             nc.vector.memset(tile[:].bitcast(I32), 0)
+        for tile in (w1s[0], w2s):
+            nc.vector.memset(tile[:].rearrange("p s i -> p (s i)").bitcast(I32), 0)
         nc.vector.memset(outs[0][:], 0.0)
 
         def load_scale_rows(tile, rows):
@@ -112,28 +105,53 @@ def tile_moe_pln_mlp_relu_kernel(
             for s in range(s0, s1):
                 w1w[e, s] = tile[:, s - s0, :]
 
+        for s in range(PASSES):
+            rows = xT[s * K_PASS : (s + 1) * K_PASS, :].rearrange("(p j) t -> p j t", j=PACK)
+            for t0, t1 in PIECES:
+                nc.sync.dma_start(out=raw[s, t0][:], in_=rows[:, :, t0:t1])
+                if s == 2 and t1 == T:
+                    load_scale_rows(w1s[0], w1_scales[0])
+                    load_w1(0, 0, 1)
+            if s == 0:
+                nc.sync.dma_start(offsets[:], offs)
+
         grouped = {}
 
-        def cast(s):
-            for t0, t1, engine in CASTS[s]:
-                name = f"grouped{s}_{t0}"
-                tag = VECTOR_CAST_TAG.get(s, name) if engine == "vector" else name
-                grouped[s, t0, t1] = keep.tile([P, (t1 - t0) * PACK], BF16, name=name, tag=tag, align_bytes=64)
-                dst = grouped[s, t0, t1][:].rearrange("p (c i t) -> p c t i", i=RUN, t=PACK)
-                src = raw[s][:, :, t0:t1].rearrange("p t (c i) -> p c t i", i=RUN)
-                if engine == "vector":
-                    nc.vector.tensor_copy(out=dst, in_=src)
-                else:
-                    nc.scalar.activation(out=dst, in_=src, func=COPY)
+        def cast(s, i):
+            t0, t1, engine, g0 = CASTS[s][i]
+            if (s, g0) not in grouped:
+                g1 = max(b for a, b, who, g in CASTS[s] if g == g0)
+                grouped[s, g0] = keep.tile([P, (g1 - g0) * PACK], BF16, name=f"grouped{s}_{g0}", align_bytes=64)
+            r0 = max(a for a, b in PIECES if a <= t0)
+            dst = grouped[s, g0][:, (t0 - g0) * PACK : (t1 - g0) * PACK].rearrange("p (c i t) -> p c t i", i=RUN, t=PACK)
+            src = raw[s, r0][:, :, t0 - r0 : t1 - r0].rearrange("p t (c i) -> p c t i", i=RUN)
+            if engine == "vector":
+                nc.vector.tensor_copy(out=dst, in_=src)
+            else:
+                nc.scalar.activation(out=dst, in_=src, func=COPY)
 
-        def quantize(s):
-            for t0, t1 in QUANTS[s]:
-                c0, c1 = [(a, b) for a, b, engine in CASTS[s] if a <= t0 and t1 <= b][0]
-                nc.vector.quantize_mx(
-                    out=words[s][:, t0:t1].bitcast(FP8X4),
-                    scales=scales[0][PACKED_ROW:P, t0:t1] if s == 1 else scales[s][:, t0:t1],
-                    in_=grouped[s, c0, c1][:, (t0 - c0) * PACK : (t1 - c0) * PACK],
-                )
+        def quantize(s, g0):
+            g1 = max(b for a, b, who, g in CASTS[s] if g == g0)
+            nc.vector.quantize_mx(
+                out=words[s][:, g0:g1].bitcast(FP8X4),
+                scales=scales[0][PACKED_ROW:P, g0:g1] if s == 1 else scales[s][:, g0:g1],
+                in_=grouped[s, g0][:],
+            )
+
+        def round_and_quantize(s):
+            if CASTS[s] == SHARED:
+                cast(s, 0)
+                cast(s, 1)
+                cast(s, 2)
+                quantize(s, 0)
+                quantize(s, 384)
+                cast(s, 3)
+                quantize(s, 256)
+                quantize(s, 512)
+            else:
+                for i in range(len(CASTS[s])):
+                    cast(s, i)
+                    quantize(s, CASTS[s][i][3])
 
         slot_words, slot_scales = {}, {}
 
@@ -155,6 +173,20 @@ def tile_moe_pln_mlp_relu_kernel(
 
         a_sums = {}
 
+        def layer1_in_quarters(e, s):
+            for q in range(PACK):
+                if s == 0:
+                    a_sums[e, q] = psum.tile([P, P], F32, name=f"a{e}_{q}", tag=QUARTER_BANKS[e][q])
+                nc.tensor.matmul_mx(
+                    out=a_sums[e, q][:],
+                    lhsT=slot_words[s, e].bitcast(FP8X4),
+                    lhsT_scale=slot_scales[s, e],
+                    rhs=w1w[e, s][:, q * 2 * P : (q + 1) * 2 * P].bitcast(FP4X4),
+                    rhs_scale=w1s[e][:, s, q * P : (q + 1) * P],
+                    start=(s == 0),
+                    stop=(s == LAST),
+                )
+
         def layer1(e, s):
             if s == 0:
                 a_sums[e] = psum.tile([P, H], F32, name=f"a{e}", tag=A_BANKS[e])
@@ -172,12 +204,21 @@ def tile_moe_pln_mlp_relu_kernel(
 
         def hidden(e):
             h_rows = keep.tile([P, H], BF16, name=f"h_rows{e}", align_bytes=64)
-            for u in range(2):
-                nc.scalar.activation(
-                    out=h_rows[:].rearrange("p (u m v) -> p u m v", u=2, v=2)[:, u],
-                    in_=a_sums[e][:].rearrange("p (m u v) -> p u m v", u=2, v=2)[:, u],
-                    func=RELU,
-                )
+            halves = h_rows[:].rearrange("p (u m v) -> p u m v", u=2, v=2)
+            if e < len(QUARTER_BANKS):
+                for q in range(PACK):
+                    nc.scalar.activation(
+                        out=halves[:, :, q * QUADRANT : (q + 1) * QUADRANT, :],
+                        in_=a_sums[e, q][:].rearrange("p (m u v) -> p u m v", u=2, v=2),
+                        func=RELU,
+                    )
+            else:
+                for u in range(2):
+                    nc.scalar.activation(
+                        out=halves[:, u],
+                        in_=a_sums[e][:].rearrange("p (m u v) -> p u m v", u=2, v=2)[:, u],
+                        func=RELU,
+                    )
             turned = psum.tile([P, 2, C], F32, name=f"turned{e}", tag=f"t{e % 2}")
             pairs = h_rows[:].bitcast(F32)
             for u in range(2):
@@ -194,13 +235,13 @@ def tile_moe_pln_mlp_relu_kernel(
                 out=h_words[e][:].bitcast(FP8X4), scales=h_scales[e][:], in_=h_grouped[e][:].bitcast(BF16)
             )
 
-        def layer2(e, half):
+        def layer2(e, unit):
             w2 = w2w[e][:, 0, :] if e < 2 else w2w_late[:, e - 2, :]
-            y_sums[e, half] = psum.tile([P, 2 * C], F32, name=f"y{e}_{half}", tag=Y_BANKS[e][half])
-            for i in range(2):
-                b = 2 * half + i
+            blocks, bank = Y_UNITS[e][unit]
+            y_sums[e, unit] = psum.tile([P, len(blocks) * C], F32, name=f"y{e}_{unit}", tag=bank)
+            for i, b in enumerate(blocks):
                 nc.tensor.matmul_mx(
-                    out=y_sums[e, half][:, i * C : (i + 1) * C],
+                    out=y_sums[e, unit][:, i * C : (i + 1) * C],
                     lhsT=w2[:, b * 2 * P : (b + 1) * 2 * P].bitcast(FP4X4),
                     lhsT_scale=w2s[:, e, b * P : (b + 1) * P],
                     rhs=h_words[e][:].bitcast(FP8X4),
@@ -209,38 +250,41 @@ def tile_moe_pln_mlp_relu_kernel(
                     stop=True,
                 )
 
-        def leave(e, half):
-            name = f"y_rows{e}_{half}"
-            tag = f"h_rows{e + 1}" if half == 1 and e + 1 < E else name
-            y_rows[e, half] = keep.tile([P, 2 * C], F32, name=name, tag=tag, align_bytes=64)
-            nc.scalar.activation(out=y_rows[e, half][:], in_=y_sums[e, half][:], func=COPY)
+        def leave(e, unit):
+            blocks, bank = Y_UNITS[e][unit]
+            name = f"y_rows{e}_{unit}"
+            tag = f"h_rows{e + 1}" if blocks[0] == 2 and e + 1 < E else name
+            rows = keep.tile([P, len(blocks) * C], F32, name=name, tag=tag, align_bytes=64)
+            nc.scalar.activation(out=rows[:], in_=y_sums[e, unit][:], func=COPY)
+            for i, b in enumerate(blocks):
+                y_rows[e, b] = rows[:, i * C : (i + 1) * C]
 
         def scatter(e, b):
             nc.vector.tensor_tensor(
                 outs[b][:].indirect(offsets[:, e * LIST_COLS : (e + 1) * LIST_COLS]),
-                y_rows[e, b // 2][:, (b % 2) * C : (b % 2 + 1) * C],
+                y_rows[e, b],
                 gates[:, e * C : (e + 1) * C],
                 MULT,
             )
             if e == E - 1:
                 nc.sync.dma_start(out=out[b * P : (b + 1) * P, :], in_=outs[b][:])
 
-        cast(0)
-        quantize(0)
+        round_and_quantize(0)
         gather_words(0, 0, E)
-        cast(1)
-        quantize(1)
+        round_and_quantize(1)
         packed = gather_scales(0, 0, E)
-
-        load_scale_rows(w1s[0], w1_scales[0])
-        load_w1(0, 0, 2)
         nc.sync.dma_start(
             out=shifted[0:SCALE_SPAN, :].bitcast(I32),
             in_=packed[PACKED_ROW : PACKED_ROW + SCALE_SPAN, :].bitcast(I32),
         )
-        load_w1(0, 2, PASSES)
-        load_scale_rows(w1s[1], w1_scales[1])
+        for e in range(E):
+            slot_scales[1, e] = shifted[:, e * C : (e + 1) * C]
+        gather_words(1, 0, E)
+
+        load_w1(0, 1, LAST)
+        load_w1(0, LAST, PASSES)
         load_w1(1, 0, LAST)
+        load_scale_rows(w1s[1], w1_scales[1])
         load_scale_rows(w2s, w2_scales[:, 0])
         load_words(w2w[0], w2_words[0])
         load_w1(1, LAST, PASSES)
@@ -251,33 +295,29 @@ def tile_moe_pln_mlp_relu_kernel(
         load_scale_rows(w1s[3], w1_scales[3])
         load_w1(3, 0, PASSES)
         load_words(w2w_late, w2_words[2:E, 0])
-        for e in range(E):
-            slot_scales[1, e] = shifted[:, e * C : (e + 1) * C]
-        gather_words(1, 0, E)
 
-        cast(2)
-        quantize(2)
+        round_and_quantize(2)
         gather_words(2, 0, 1)
         gather_scales(2, 0, 1)
-        cast(LAST)
-        quantize(LAST)
+        gather_words(2, 1, 2)
+        round_and_quantize(LAST)
         for e in range(2):
             gather_words(LAST, e, e + 1)
             gather_scales(LAST, e, e + 1)
-        gather_scales(LAST, 2, E)
         for s in range(PASSES):
-            layer1(0, s)
+            layer1_in_quarters(0, s)
 
-        gather_words(2, 1, 2, tag="slot_scales3_0")
-        gather_scales(2, 1, 2, tag="slot_words3_0")
+        gather_scales(2, 1, 2, tag="grouped3_512")
+        gather_scales(LAST, 2, E)
+        gather_scales(2, 2, E, tag="slot_scales3_0")
         hidden(0)
-        gather_scales(2, 2, E, tag="w1w0_2")
         for s in range(LAST):
-            layer1(1, s)
+            layer1_in_quarters(1, s)
         hidden_quantize(0)
-        layer2(0, 0)
-        leave(0, 0)
-        layer1(1, LAST)
+        for unit in range(2):
+            layer2(0, unit)
+            leave(0, unit)
+        layer1_in_quarters(1, LAST)
 
         late = keep.tile([P, 4 * C], U32, name="late_words", tag="h_grouped0", align_bytes=64)
         gather(words[2][:].bitcast(U32), slot_words, 2, 2, E, late[:, 0 : 2 * C])
@@ -287,8 +327,8 @@ def tile_moe_pln_mlp_relu_kernel(
             if e + 1 < E:
                 hidden(e + 1)
             if e == 0:
-                layer2(0, 1)
-            leave(e, 1)
+                layer2(0, 2)
+            leave(e, len(Y_UNITS[e]) - 1)
             scatter(e, 0)
             scatter(e, 1)
             if e + 2 < E:

@@ -32,14 +32,22 @@ COPY = mybir.ActivationFunctionType.Copy
 RELU = mybir.ActivationFunctionType.Relu
 MULT = mybir.AluOpType.mult
 
-PIECES = ((0, 256), (256, 512), (512, 640))
-SHARED = ((0, 256, "scalar", 0), (256, 384, "scalar", 256), (384, 512, "vector", 384), (512, 640, "vector", 512))
-SCALAR_ALONE = ((0, 256, "scalar", 0), (256, 512, "scalar", 256), (512, 640, "scalar", 512))
-LAST_ON_VECTOR = ((0, 256, "scalar", 0), (512, 640, "vector", 512), (256, 512, "scalar", 256))
-CASTS = (SHARED, SHARED, SCALAR_ALONE, SHARED)
+CASTS = (
+    ((0, 256, "vector"), (256, 384, "vector"), (384, 640, "scalar")),
+    ((0, 256, "vector"), (256, 384, "vector"), (384, 512, "scalar"), (512, 640, "scalar")),
+    ((0, 256, "scalar"), (256, 384, "scalar"), (384, 512, "vector"), (512, 640, "scalar")),
+    ((0, 128, "scalar"), (128, 256, "vector"), (256, 384, "vector"), (384, 512, "scalar"), (512, 640, "scalar")),
+)
+QUANTS = (
+    ((0, 256), (256, 384), (384, 640)),
+    ((384, 512), (0, 256), (256, 384), (512, 640)),
+    ((0, 256), (256, 512), (512, 640)),
+    ((0, 256), (256, 512), (512, 640)),
+)
+PASS_ORDER = ((0, 1, 2, 3), (0, 1, 2, 3))
 Y_UNITS = (
-    (((0,), "y0_0"), ((1,), "y3_1"), ((2, 3), "a1")),
-    (((0, 1), "y1_0"), ((2, 3), "y1_1")),
+    (((0,), "y0_0"), ((1, 2), "y3_1"), ((3,), "a1")),
+    (((0,), "y1_0"), ((1,), "a0"), ((2, 3), "y1_1")),
     (((0, 1), "a0"), ((2, 3), "a1")),
     (((0, 1), "t0"), ((2, 3), "y3_1")),
 )
@@ -57,9 +65,7 @@ def tile_moe_pln_mlp_relu_kernel(
 
         offsets = keep.tile([P, SLOTS // 16], U16, name="offsets")
 
-        raw = {
-            (s, t0): keep.tile([P, PACK, t1 - t0], F32, name=f"raw{s}_{t0}") for s in range(PASSES) for t0, t1 in PIECES
-        }
+        raw = [keep.tile([P, PACK, T], F32, name=f"raw{s}", align_bytes=64) for s in range(PASSES)]
         words = [keep.tile([P, WINDOW], I32, name=f"words{s}", align_bytes=64) for s in range(PASSES)]
         scales = {s: keep.tile([P, WINDOW], U8, name=f"scales{s}", align_bytes=64) for s in (0, 2, 3)}
         shifted = keep.tile([P, SLOTS], U8, name="shifted", align_bytes=64)
@@ -67,10 +73,10 @@ def tile_moe_pln_mlp_relu_kernel(
         w2w = [keep.tile([P, 1, 2 * N], U8, name=f"w2w{e}", align_bytes=64) for e in range(2)]
         w2w_late = keep.tile([P, 2, 2 * N], U8, name="w2w_late", align_bytes=64)
         w2s = keep.tile([P, E, N], U8, name="w2s", align_bytes=64)
-        gates = keep.tile([P, SLOTS], F32, name="gates")
         outs = [keep.tile([P, T], F32, name=f"outs{b}") for b in range(BLOCKS)]
         ident = keep.tile([P, P], F32, name="ident")
         zero = keep.tile([P, 1], F32, name="zero")
+        gates = keep.tile([P, SLOTS], F32, name="gates")
 
         nc.vector.memset(zero[:], 0.0)
         for b in range(2, BLOCKS):
@@ -106,52 +112,31 @@ def tile_moe_pln_mlp_relu_kernel(
                 w1w[e, s] = tile[:, s - s0, :]
 
         for s in range(PASSES):
-            rows = xT[s * K_PASS : (s + 1) * K_PASS, :].rearrange("(p j) t -> p j t", j=PACK)
-            for t0, t1 in PIECES:
-                nc.sync.dma_start(out=raw[s, t0][:], in_=rows[:, :, t0:t1])
-                if s == 2 and t1 == T:
-                    load_scale_rows(w1s[0], w1_scales[0])
-                    load_w1(0, 0, 1)
+            nc.sync.dma_start(
+                out=raw[s][:], in_=xT[s * K_PASS : (s + 1) * K_PASS, :].rearrange("(p j) t -> p j t", j=PACK)
+            )
             if s == 0:
                 nc.sync.dma_start(offsets[:], offs)
 
         grouped = {}
 
-        def cast(s, i):
-            t0, t1, engine, g0 = CASTS[s][i]
-            if (s, g0) not in grouped:
-                g1 = max(b for a, b, who, g in CASTS[s] if g == g0)
-                grouped[s, g0] = keep.tile([P, (g1 - g0) * PACK], BF16, name=f"grouped{s}_{g0}", align_bytes=64)
-            r0 = max(a for a, b in PIECES if a <= t0)
-            dst = grouped[s, g0][:, (t0 - g0) * PACK : (t1 - g0) * PACK].rearrange("p (c i t) -> p c t i", i=RUN, t=PACK)
-            src = raw[s, r0][:, :, t0 - r0 : t1 - r0].rearrange("p t (c i) -> p c t i", i=RUN)
-            if engine == "vector":
-                nc.vector.tensor_copy(out=dst, in_=src)
-            else:
-                nc.scalar.activation(out=dst, in_=src, func=COPY)
-
-        def quantize(s, g0):
-            g1 = max(b for a, b, who, g in CASTS[s] if g == g0)
-            nc.vector.quantize_mx(
-                out=words[s][:, g0:g1].bitcast(FP8X4),
-                scales=scales[0][PACKED_ROW:P, g0:g1] if s == 1 else scales[s][:, g0:g1],
-                in_=grouped[s, g0][:],
-            )
-
         def round_and_quantize(s):
-            if CASTS[s] == SHARED:
-                cast(s, 0)
-                cast(s, 1)
-                cast(s, 2)
-                quantize(s, 0)
-                quantize(s, 384)
-                cast(s, 3)
-                quantize(s, 256)
-                quantize(s, 512)
-            else:
-                for i in range(len(CASTS[s])):
-                    cast(s, i)
-                    quantize(s, CASTS[s][i][3])
+            for q0, q1 in QUANTS[s]:
+                grouped[s, q0] = keep.tile([P, (q1 - q0) * PACK], BF16, name=f"grouped{s}_{q0}", align_bytes=64)
+            for t0, t1, engine in CASTS[s]:
+                q0 = [a for a, b in QUANTS[s] if a <= t0 and t1 <= b][0]
+                dst = grouped[s, q0][:, (t0 - q0) * PACK : (t1 - q0) * PACK].rearrange("p (c i t) -> p c t i", i=RUN, t=PACK)
+                src = raw[s][:, :, t0:t1].rearrange("p t (c i) -> p c t i", i=RUN)
+                if engine == "vector":
+                    nc.vector.tensor_copy(out=dst, in_=src)
+                else:
+                    nc.scalar.activation(out=dst, in_=src, func=COPY)
+            for t0, t1 in QUANTS[s]:
+                nc.vector.quantize_mx(
+                    out=words[s][:, t0:t1].bitcast(FP8X4),
+                    scales=scales[0][PACKED_ROW:P, t0:t1] if s == 1 else scales[s][:, t0:t1],
+                    in_=grouped[s, t0][:],
+                )
 
         slot_words, slot_scales = {}, {}
 
@@ -173,9 +158,10 @@ def tile_moe_pln_mlp_relu_kernel(
 
         a_sums = {}
 
-        def layer1_in_quarters(e, s):
+        def layer1_in_quarters(e, i):
+            s = PASS_ORDER[e][i]
             for q in range(PACK):
-                if s == 0:
+                if i == 0:
                     a_sums[e, q] = psum.tile([P, P], F32, name=f"a{e}_{q}", tag=QUARTER_BANKS[e][q])
                 nc.tensor.matmul_mx(
                     out=a_sums[e, q][:],
@@ -183,8 +169,8 @@ def tile_moe_pln_mlp_relu_kernel(
                     lhsT_scale=slot_scales[s, e],
                     rhs=w1w[e, s][:, q * 2 * P : (q + 1) * 2 * P].bitcast(FP4X4),
                     rhs_scale=w1s[e][:, s, q * P : (q + 1) * P],
-                    start=(s == 0),
-                    stop=(s == LAST),
+                    start=(i == 0),
+                    stop=(i == LAST),
                 )
 
         def layer1(e, s):
@@ -253,7 +239,7 @@ def tile_moe_pln_mlp_relu_kernel(
         def leave(e, unit):
             blocks, bank = Y_UNITS[e][unit]
             name = f"y_rows{e}_{unit}"
-            tag = f"h_rows{e + 1}" if blocks[0] == 2 and e + 1 < E else name
+            tag = f"h_rows{e + 1}" if blocks[-1] == BLOCKS - 1 and e + 1 < E else name
             rows = keep.tile([P, len(blocks) * C], F32, name=name, tag=tag, align_bytes=64)
             nc.scalar.activation(out=rows[:], in_=y_sums[e, unit][:], func=COPY)
             for i, b in enumerate(blocks):
@@ -270,21 +256,23 @@ def tile_moe_pln_mlp_relu_kernel(
                 nc.sync.dma_start(out=out[b * P : (b + 1) * P, :], in_=outs[b][:])
 
         round_and_quantize(0)
-        gather_words(0, 0, E)
+        gather_words(0, 0, E - 1)
         round_and_quantize(1)
+        gather_words(0, E - 1, E, tag="grouped1_256")
         packed = gather_scales(0, 0, E)
-        nc.sync.dma_start(
-            out=shifted[0:SCALE_SPAN, :].bitcast(I32),
-            in_=packed[PACKED_ROW : PACKED_ROW + SCALE_SPAN, :].bitcast(I32),
-        )
         for e in range(E):
             slot_scales[1, e] = shifted[:, e * C : (e + 1) * C]
         gather_words(1, 0, E)
 
-        load_w1(0, 1, LAST)
-        load_w1(0, LAST, PASSES)
-        load_w1(1, 0, LAST)
+        load_scale_rows(w1s[0], w1_scales[0])
+        load_w1(0, 0, 2)
+        nc.sync.dma_start(
+            out=shifted[0:SCALE_SPAN, :].bitcast(I32),
+            in_=packed[PACKED_ROW : PACKED_ROW + SCALE_SPAN, :].bitcast(I32),
+        )
+        load_w1(0, 2, PASSES)
         load_scale_rows(w1s[1], w1_scales[1])
+        load_w1(1, 0, LAST)
         load_scale_rows(w2s, w2_scales[:, 0])
         load_words(w2w[0], w2_words[0])
         load_w1(1, LAST, PASSES)
@@ -299,18 +287,18 @@ def tile_moe_pln_mlp_relu_kernel(
         round_and_quantize(2)
         gather_words(2, 0, 1)
         gather_scales(2, 0, 1)
-        gather_words(2, 1, 2)
         round_and_quantize(LAST)
-        for e in range(2):
-            gather_words(LAST, e, e + 1)
-            gather_scales(LAST, e, e + 1)
+        gather_words(LAST, 0, 1)
+        gather_scales(LAST, 0, 1)
         for s in range(PASSES):
             layer1_in_quarters(0, s)
 
-        gather_scales(2, 1, 2, tag="grouped3_512")
-        gather_scales(LAST, 2, E)
-        gather_scales(2, 2, E, tag="slot_scales3_0")
+        gather_words(2, 1, 2, tag="grouped3_512")
+        gather_words(LAST, 1, 2)
+        gather_scales(LAST, 1, E)
+        gather_scales(2, 1, E, tag="slot_scales3_0")
         hidden(0)
+        gather_words(2, 2, 3, tag="h_rows0")
         for s in range(LAST):
             layer1_in_quarters(1, s)
         hidden_quantize(0)
@@ -319,25 +307,27 @@ def tile_moe_pln_mlp_relu_kernel(
             leave(0, unit)
         layer1_in_quarters(1, LAST)
 
-        late = keep.tile([P, 4 * C], U32, name="late_words", tag="h_grouped0", align_bytes=64)
-        gather(words[2][:].bitcast(U32), slot_words, 2, 2, E, late[:, 0 : 2 * C])
-        gather(words[LAST][:].bitcast(U32), slot_words, LAST, 2, E, late[:, 2 * C :])
+        late = keep.tile([P, 3 * C], U32, name="late_words", tag="h_grouped0", align_bytes=64)
+        gather(words[LAST][:].bitcast(U32), slot_words, LAST, 2, E, late[:, 0 : 2 * C])
+        gather(words[2][:].bitcast(U32), slot_words, 2, 3, E, late[:, 2 * C :])
 
         for e in range(E):
+            held = len(Y_UNITS[e]) - 1
             if e + 1 < E:
                 hidden(e + 1)
             if e == 0:
-                layer2(0, 2)
-            leave(e, len(Y_UNITS[e]) - 1)
-            scatter(e, 0)
-            scatter(e, 1)
+                layer2(0, held)
+            leave(e, held)
+            for b in range(Y_UNITS[e][held][0][0]):
+                scatter(e, b)
             if e + 2 < E:
                 for s in range(PASSES):
                     layer1(e + 2, s)
             if e + 1 < E:
                 hidden_quantize(e + 1)
-                layer2(e + 1, 0)
-                leave(e + 1, 0)
-                layer2(e + 1, 1)
-            scatter(e, 2)
-            scatter(e, 3)
+                for unit in range(len(Y_UNITS[e + 1]) - 1):
+                    layer2(e + 1, unit)
+                    leave(e + 1, unit)
+                layer2(e + 1, len(Y_UNITS[e + 1]) - 1)
+            for b in Y_UNITS[e][held][0]:
+                scatter(e, b)

@@ -35,7 +35,7 @@ MULT = mybir.AluOpType.mult
 CASTS = (
     ((0, 256, "vector"), (256, 384, "vector"), (384, 640, "scalar")),
     ((0, 256, "vector"), (256, 384, "vector"), (384, 512, "scalar"), (512, 640, "scalar")),
-    ((0, 256, "scalar"), (256, 384, "scalar"), (384, 512, "vector"), (512, 640, "scalar")),
+    ((0, 256, "scalar"), (256, 384, "scalar"), (384, 512, "gpsimd"), (512, 640, "scalar")),
     ((0, 128, "scalar"), (128, 256, "vector"), (256, 384, "vector"), (384, 512, "scalar"), (512, 640, "scalar")),
 )
 QUANTS = (
@@ -129,6 +129,8 @@ def tile_moe_pln_mlp_relu_kernel(
                 src = raw[s][:, :, t0:t1].rearrange("p t (c i) -> p c t i", i=RUN)
                 if engine == "vector":
                     nc.vector.tensor_copy(out=dst, in_=src)
+                elif engine == "gpsimd":
+                    nc.gpsimd.tensor_copy(out=dst, in_=src)
                 else:
                     nc.scalar.activation(out=dst, in_=src, func=COPY)
             for t0, t1 in QUANTS[s]:

@@ -44,15 +44,7 @@ QUANTS = (
     ((0, 256), (256, 512), (512, 640)),
     ((0, 256), (256, 512), (512, 640)),
 )
-PASS_ORDER = ((0, 1, 2, 3), (0, 1, 2, 3))
-Y_UNITS = (
-    (((0,), "y0_0"), ((1, 2), "y3_1"), ((3,), "a1")),
-    (((0,), "y1_0"), ((1,), "a0"), ((2, 3), "y1_1")),
-    (((0, 1), "a0"), ((2, 3), "a1")),
-    (((0, 1), "t0"), ((2, 3), "y3_1")),
-)
-QUARTER_BANKS = (("a0", "y1_1", "y3_1", "t1"), ("a1", "y1_0", "a0", "y1_1"))
-A_BANKS = ("a0", "a1", "y0_0", "y1_0")
+QUARTER_BANKS = ("a0", "v1", "s1", "t1")
 
 
 def tile_moe_pln_mlp_relu_kernel(
@@ -160,51 +152,36 @@ def tile_moe_pln_mlp_relu_kernel(
 
         a_sums = {}
 
-        def layer1_in_quarters(e, i):
-            s = PASS_ORDER[e][i]
-            for q in range(PACK):
-                if i == 0:
-                    a_sums[e, q] = psum.tile([P, P], F32, name=f"a{e}_{q}", tag=QUARTER_BANKS[e][q])
-                nc.tensor.matmul_mx(
-                    out=a_sums[e, q][:],
-                    lhsT=slot_words[s, e].bitcast(FP8X4),
-                    lhsT_scale=slot_scales[s, e],
-                    rhs=w1w[e, s][:, q * 2 * P : (q + 1) * 2 * P].bitcast(FP4X4),
-                    rhs_scale=w1s[e][:, s, q * P : (q + 1) * P],
-                    start=(i == 0),
-                    stop=(i == LAST),
-                )
-
-        def layer1(e, s):
+        def layer1(e, s, bank, c0, c1):
             if s == 0:
-                a_sums[e] = psum.tile([P, H], F32, name=f"a{e}", tag=A_BANKS[e])
+                a_sums[e, c0] = psum.tile([P, c1 - c0], F32, name=f"a{e}_{c0}", tag=bank)
             nc.tensor.matmul_mx(
-                out=a_sums[e][:],
+                out=a_sums[e, c0][:],
                 lhsT=slot_words[s, e].bitcast(FP8X4),
                 lhsT_scale=slot_scales[s, e],
-                rhs=w1w[e, s].bitcast(FP4X4),
-                rhs_scale=w1s[e][:, s, :],
+                rhs=w1w[e, s][:, 2 * c0 : 2 * c1].bitcast(FP4X4),
+                rhs_scale=w1s[e][:, s, c0:c1],
                 start=(s == 0),
                 stop=(s == LAST),
             )
 
-        h_grouped, h_words, h_scales, y_sums, y_rows = {}, {}, {}, {}, {}
+        h_grouped, h_words, h_scales = {}, {}, {}
 
         def hidden(e):
             h_rows = keep.tile([P, H], BF16, name=f"h_rows{e}", align_bytes=64)
             halves = h_rows[:].rearrange("p (u m v) -> p u m v", u=2, v=2)
-            if e < len(QUARTER_BANKS):
+            if e == 0:
                 for q in range(PACK):
                     nc.scalar.activation(
                         out=halves[:, :, q * QUADRANT : (q + 1) * QUADRANT, :],
-                        in_=a_sums[e, q][:].rearrange("p (m u v) -> p u m v", u=2, v=2),
+                        in_=a_sums[e, q * P][:].rearrange("p (m u v) -> p u m v", u=2, v=2),
                         func=RELU,
                     )
             else:
                 for u in range(2):
                     nc.scalar.activation(
                         out=halves[:, u],
-                        in_=a_sums[e][:].rearrange("p (m u v) -> p u m v", u=2, v=2)[:, u],
+                        in_=a_sums[e, 0][:].rearrange("p (m u v) -> p u m v", u=2, v=2)[:, u],
                         func=RELU,
                     )
             turned = psum.tile([P, 2, C], F32, name=f"turned{e}", tag=f"t{e % 2}")
@@ -223,38 +200,44 @@ def tile_moe_pln_mlp_relu_kernel(
                 out=h_words[e][:].bitcast(FP8X4), scales=h_scales[e][:], in_=h_grouped[e][:].bitcast(BF16)
             )
 
-        def layer2(e, unit):
+        y_sums = {}
+
+        def layer2(e):
             w2 = w2w[e][:, 0, :] if e < 2 else w2w_late[:, e - 2, :]
-            blocks, bank = Y_UNITS[e][unit]
-            y_sums[e, unit] = psum.tile([P, len(blocks) * C], F32, name=f"y{e}_{unit}", tag=bank)
-            for i, b in enumerate(blocks):
-                nc.tensor.matmul_mx(
-                    out=y_sums[e, unit][:, i * C : (i + 1) * C],
-                    lhsT=w2[:, b * 2 * P : (b + 1) * 2 * P].bitcast(FP4X4),
-                    lhsT_scale=w2s[:, e, b * P : (b + 1) * P],
-                    rhs=h_words[e][:].bitcast(FP8X4),
-                    rhs_scale=h_scales[e][:],
-                    start=True,
-                    stop=True,
-                )
+            for half, bank in enumerate(("v", "s")):
+                y_sums[e, half] = psum.tile([P, 2, C], F32, name=f"y{e}_{bank}", tag=f"{bank}{e % 2}")
+                for i in range(2):
+                    b = 2 * half + i
+                    nc.tensor.matmul_mx(
+                        out=y_sums[e, half][:, i, :],
+                        lhsT=w2[:, b * 2 * P : (b + 1) * 2 * P].bitcast(FP4X4),
+                        lhsT_scale=w2s[:, e, b * P : (b + 1) * P],
+                        rhs=h_words[e][:].bitcast(FP8X4),
+                        rhs_scale=h_scales[e][:],
+                        start=True,
+                        stop=True,
+                    )
 
-        def leave(e, unit):
-            blocks, bank = Y_UNITS[e][unit]
-            name = f"y_rows{e}_{unit}"
-            tag = f"h_rows{e + 1}" if blocks[-1] == BLOCKS - 1 and e + 1 < E else name
-            rows = keep.tile([P, len(blocks) * C], F32, name=name, tag=tag, align_bytes=64)
-            nc.scalar.activation(out=rows[:], in_=y_sums[e, unit][:], func=COPY)
-            for i, b in enumerate(blocks):
-                y_rows[e, b] = rows[:, i * C : (i + 1) * C]
+        y_rows = {}
 
-        def scatter(e, b):
+        def leave(e, half, rows):
             nc.vector.tensor_tensor(
-                outs[b][:].indirect(offsets[:, e * LIST_COLS : (e + 1) * LIST_COLS]),
-                y_rows[e, b],
-                gates[:, e * C : (e + 1) * C],
-                MULT,
+                rows, y_sums[e, half][:], gates[:, e * C : (e + 1) * C].unsqueeze(1).to_broadcast([P, 2, C]), MULT
             )
-            if e == E - 1:
+
+        def rows_tile(e0, e1, half, tag=None):
+            name = f"y_rows{e0}_{half}"
+            rows = keep.tile([P, 2, (e1 - e0) * C], F32, name=name, tag=tag or name, align_bytes=64)
+            y_rows[e0, 2 * half], y_rows[e0, 2 * half + 1] = rows[:, 0, :], rows[:, 1, :]
+            return rows
+
+        def scatter(e0, e1, b):
+            window = outs[b][:].indirect(offsets[:, e0 * LIST_COLS : e1 * LIST_COLS])
+            if b % 2 == 0:
+                nc.vector.tensor_copy(out=window, in_=y_rows[e0, b])
+            else:
+                nc.scalar.activation(out=window, in_=y_rows[e0, b], func=COPY)
+            if e1 == E:
                 nc.sync.dma_start(out=out[b * P : (b + 1) * P, :], in_=outs[b][:])
 
         round_and_quantize(0)
@@ -276,11 +259,12 @@ def tile_moe_pln_mlp_relu_kernel(
         load_scale_rows(w1s[1], w1_scales[1])
         load_w1(1, 0, LAST)
         load_scale_rows(w2s, w2_scales[:, 0])
-        load_words(w2w[0], w2_words[0])
         load_w1(1, LAST, PASSES)
+        load_words(w2w[0], w2_words[0])
         nc.sync.dma_start(out=gates[:], in_=gate[0:P, :])
         load_scale_rows(w1s[2], w1_scales[2])
-        load_w1(2, 0, PASSES)
+        load_w1(2, 0, 2)
+        load_w1(2, 2, PASSES)
         load_words(w2w[1], w2_words[1])
         load_scale_rows(w1s[3], w1_scales[3])
         load_w1(3, 0, PASSES)
@@ -293,43 +277,51 @@ def tile_moe_pln_mlp_relu_kernel(
         gather_words(LAST, 0, 1)
         gather_scales(LAST, 0, 1)
         for s in range(PASSES):
-            layer1_in_quarters(0, s)
-
+            for q in range(PACK):
+                layer1(0, s, QUARTER_BANKS[q], q * P, (q + 1) * P)
         gather_words(2, 1, 2, tag="grouped3_512")
         gather_words(LAST, 1, 2)
-        gather_scales(LAST, 1, E)
+        gather_scales(LAST, 1, 2)
         gather_scales(2, 1, E, tag="slot_scales3_0")
         hidden(0)
         gather_words(2, 2, 3, tag="h_rows0")
-        for s in range(LAST):
-            layer1_in_quarters(1, s)
+        for s in range(PASSES):
+            layer1(1, s, "a1", 0, H)
         hidden_quantize(0)
-        for unit in range(2):
-            layer2(0, unit)
-            leave(0, unit)
-        layer1_in_quarters(1, LAST)
+        gather_scales(LAST, 2, E, tag="h_grouped0")
 
-        late = keep.tile([P, 3 * C], U32, name="late_words", tag="h_grouped0", align_bytes=64)
-        gather(words[LAST][:].bitcast(U32), slot_words, LAST, 2, E, late[:, 0 : 2 * C])
-        gather(words[2][:].bitcast(U32), slot_words, 2, 3, E, late[:, 2 * C :])
-
-        for e in range(E):
-            held = len(Y_UNITS[e]) - 1
-            if e + 1 < E:
-                hidden(e + 1)
+        layer2(0)
+        gather_words(LAST, 2, 3, tag="h_words0")
+        for e in range(2):
+            hidden(e + 1)
+            leave(e, 0, rows_tile(e, e + 1, 0, tag=f"h_rows{e + 1}")[:])
+            hidden_quantize(e + 1)
+            scatter(e, e + 1, 0)
+            scatter(e, e + 1, 1)
+            for s in range(PASSES):
+                layer1(e + 2, s, f"a{e % 2}", 0, H)
+            leave(e, 1, rows_tile(e, e + 1, 1, tag=("w1w2_2", "w1w3_0")[e])[:])
             if e == 0:
-                layer2(0, held)
-            leave(e, held)
-            for b in range(Y_UNITS[e][held][0][0]):
-                scatter(e, b)
-            if e + 2 < E:
-                for s in range(PASSES):
-                    layer1(e + 2, s)
-            if e + 1 < E:
-                hidden_quantize(e + 1)
-                for unit in range(len(Y_UNITS[e + 1]) - 1):
-                    layer2(e + 1, unit)
-                    leave(e + 1, unit)
-                layer2(e + 1, len(Y_UNITS[e + 1]) - 1)
-            for b in Y_UNITS[e][held][0]:
-                scatter(e, b)
+                late = keep.tile([P, 2 * C], U32, name="late_words", tag="h_words0", align_bytes=64)
+                gather(words[2][:].bitcast(U32), slot_words, 2, 3, E, late[:, :C])
+                gather(words[LAST][:].bitcast(U32), slot_words, LAST, 3, E, late[:, C:])
+            scatter(e, e + 1, 2)
+            scatter(e, e + 1, 3)
+            layer2(e + 1)
+        hidden(3)
+        rows = keep.tile([P, 3, 2, C], F32, name="y_rows_last", tag="h_rows3", align_bytes=64)
+        leave(2, 0, rows[:, 0])
+        leave(2, 1, rows[:, 1:, 0, :])
+        hidden_quantize(3)
+        y_rows[2, 0], y_rows[2, 1], y_rows[2, 3], y_rows[3, 3] = rows[:, 0, 0], rows[:, 0, 1], rows[:, 2, 0], rows[:, 2, 1]
+        y_rows[2, 2] = rows[:, 1].rearrange("p e c -> p (e c)")
+        scatter(2, 3, 0)
+        scatter(2, 3, 1)
+        scatter(2, 3, 3)
+        layer2(3)
+        leave(3, 0, rows_tile(3, E, 0)[:])
+        leave(3, 1, rows[:, 1:, 1, :])
+        scatter(3, E, 1)
+        scatter(3, E, 0)
+        scatter(3, E, 3)
+        scatter(2, E, 2)

@@ -189,12 +189,11 @@ def tile_moe_pln_mlp_relu_kernel(
             for u in range(2):
                 nc.tensor.transpose(turned[:, u, :], pairs[:, u * P : (u + 1) * P], ident[:])
             h_grouped[e] = keep.tile([P, 2 * C], F32, name=f"h_grouped{e}", align_bytes=64)
-            nc.scalar.copy(
-                out=h_grouped[e][:].rearrange("p (c u) -> p c u", u=2), in_=turned[:].rearrange("p u c -> p c u")
-            )
+            copy = nc.vector.tensor_copy if e == 1 else nc.scalar.copy
+            copy(out=h_grouped[e][:].rearrange("p (c u) -> p c u", u=2), in_=turned[:].rearrange("p u c -> p c u"))
 
-        def hidden_quantize(e):
-            h_words[e] = keep.tile([P, C], U32, name=f"h_words{e}", align_bytes=64)
+        def hidden_quantize(e, tag=None):
+            h_words[e] = keep.tile([P, C], U32, name=f"h_words{e}", tag=tag or f"h_words{e}", align_bytes=64)
             h_scales[e] = keep.tile([P, C], U8, name=f"h_scales{e}", align_bytes=64)
             nc.vector.quantize_mx(
                 out=h_words[e][:].bitcast(FP8X4), scales=h_scales[e][:], in_=h_grouped[e][:].bitcast(BF16)
@@ -202,42 +201,40 @@ def tile_moe_pln_mlp_relu_kernel(
 
         y_sums = {}
 
-        def layer2(e):
+        def layer2(e, b0, b1, bank):
             w2 = w2w[e][:, 0, :] if e < 2 else w2w_late[:, e - 2, :]
-            for half, bank in enumerate(("v", "s")):
-                y_sums[e, half] = psum.tile([P, 2, C], F32, name=f"y{e}_{bank}", tag=f"{bank}{e % 2}")
-                for i in range(2):
-                    b = 2 * half + i
-                    nc.tensor.matmul_mx(
-                        out=y_sums[e, half][:, i, :],
-                        lhsT=w2[:, b * 2 * P : (b + 1) * 2 * P].bitcast(FP4X4),
-                        lhsT_scale=w2s[:, e, b * P : (b + 1) * P],
-                        rhs=h_words[e][:].bitcast(FP8X4),
-                        rhs_scale=h_scales[e][:],
-                        start=True,
-                        stop=True,
-                    )
+            sums = psum.tile([P, b1 - b0, C], F32, name=f"y{e}_{b0}", tag=bank)
+            for b in range(b0, b1):
+                y_sums[e, b] = (sums, b - b0)
+                nc.tensor.matmul_mx(
+                    out=sums[:, b - b0, :],
+                    lhsT=w2[:, b * 2 * P : (b + 1) * 2 * P].bitcast(FP4X4),
+                    lhsT_scale=w2s[:, e, b * P : (b + 1) * P],
+                    rhs=h_words[e][:].bitcast(FP8X4),
+                    rhs_scale=h_scales[e][:],
+                    start=True,
+                    stop=True,
+                )
 
-        y_rows = {}
-
-        def leave(e, half, rows):
+        def leave(e, b0, b1, rows):
+            sums, i = y_sums[e, b0]
             nc.vector.tensor_tensor(
-                rows, y_sums[e, half][:], gates[:, e * C : (e + 1) * C].unsqueeze(1).to_broadcast([P, 2, C]), MULT
+                rows,
+                sums[:, i : i + b1 - b0, :],
+                gates[:, e * C : (e + 1) * C].unsqueeze(1).to_broadcast([P, b1 - b0, C]),
+                MULT,
             )
 
-        def rows_tile(e0, e1, half, tag=None):
-            name = f"y_rows{e0}_{half}"
-            rows = keep.tile([P, 2, (e1 - e0) * C], F32, name=name, tag=tag or name, align_bytes=64)
-            y_rows[e0, 2 * half], y_rows[e0, 2 * half + 1] = rows[:, 0, :], rows[:, 1, :]
-            return rows
+        def rows_tile(name, blocks, slots, tag=None):
+            return keep.tile([P, blocks, slots], F32, name=name, tag=tag or name, align_bytes=64)
 
-        def scatter(e0, e1, b):
-            window = outs[b][:].indirect(offsets[:, e0 * LIST_COLS : e1 * LIST_COLS])
-            if b % 2 == 0:
-                nc.vector.tensor_copy(out=window, in_=y_rows[e0, b])
+        def scatter(engine, b, j0, j1, rows):
+            window = outs[b][:].indirect(offsets[:, j0 // 16 : j1 // 16])
+            if engine == "vector":
+                nc.vector.tensor_copy(out=window, in_=rows)
             else:
-                nc.scalar.activation(out=window, in_=y_rows[e0, b], func=COPY)
-            if e1 == E:
+                nc.scalar.activation(out=window, in_=rows, func=COPY)
+            if j1 == SLOTS:
                 nc.sync.dma_start(out=out[b * P : (b + 1) * P, :], in_=outs[b][:])
 
         round_and_quantize(0)
@@ -250,25 +247,27 @@ def tile_moe_pln_mlp_relu_kernel(
         gather_words(1, 0, E)
 
         load_scale_rows(w1s[0], w1_scales[0])
-        load_w1(0, 0, 2)
+        load_w1(0, 0, LAST)
         nc.sync.dma_start(
             out=shifted[0:SCALE_SPAN, :].bitcast(I32),
             in_=packed[PACKED_ROW : PACKED_ROW + SCALE_SPAN, :].bitcast(I32),
         )
-        load_w1(0, 2, PASSES)
         load_scale_rows(w1s[1], w1_scales[1])
-        load_w1(1, 0, LAST)
+        load_w1(0, LAST, PASSES)
+        load_w1(1, 0, 2)
         load_scale_rows(w2s, w2_scales[:, 0])
-        load_w1(1, LAST, PASSES)
+        nc.sync.dma_start(out=gates[:, : 2 * C], in_=gate[0:P, : 2 * C])
+        load_w1(1, 2, PASSES)
         load_words(w2w[0], w2_words[0])
-        nc.sync.dma_start(out=gates[:], in_=gate[0:P, :])
         load_scale_rows(w1s[2], w1_scales[2])
         load_w1(2, 0, 2)
         load_w1(2, 2, PASSES)
         load_words(w2w[1], w2_words[1])
         load_scale_rows(w1s[3], w1_scales[3])
-        load_w1(3, 0, PASSES)
+        load_w1(3, 0, 2)
+        load_w1(3, 2, PASSES)
         load_words(w2w_late, w2_words[2:E, 0])
+        nc.sync.dma_start(out=gates[:, 2 * C :], in_=gate[0:P, 2 * C :])
 
         round_and_quantize(2)
         gather_words(2, 0, 1)
@@ -282,7 +281,8 @@ def tile_moe_pln_mlp_relu_kernel(
         gather_words(2, 1, 2, tag="grouped3_512")
         gather_words(LAST, 1, 2)
         gather_scales(LAST, 1, 2)
-        gather_scales(2, 1, E, tag="slot_scales3_0")
+        gather_scales(2, 1, 2, tag="slot_words3_0")
+        gather_scales(2, 2, E, tag="slot_scales3_0")
         hidden(0)
         gather_words(2, 2, 3, tag="h_rows0")
         for s in range(PASSES):
@@ -290,38 +290,54 @@ def tile_moe_pln_mlp_relu_kernel(
         hidden_quantize(0)
         gather_scales(LAST, 2, E, tag="h_grouped0")
 
-        layer2(0)
+        layer2(0, 0, 2, "v0")
+        layer2(0, 2, BLOCKS, "s0")
+        hidden(1)
+        rows = rows_tile("y_rows0_0", 2, C)
+        leave(0, 0, 2, rows[:])
         gather_words(LAST, 2, 3, tag="h_words0")
-        for e in range(2):
-            hidden(e + 1)
-            leave(e, 0, rows_tile(e, e + 1, 0, tag=f"h_rows{e + 1}")[:])
-            hidden_quantize(e + 1)
-            scatter(e, e + 1, 0)
-            scatter(e, e + 1, 1)
-            for s in range(PASSES):
-                layer1(e + 2, s, f"a{e % 2}", 0, H)
-            leave(e, 1, rows_tile(e, e + 1, 1, tag=("w1w2_2", "w1w3_0")[e])[:])
-            if e == 0:
-                late = keep.tile([P, 2 * C], U32, name="late_words", tag="h_words0", align_bytes=64)
-                gather(words[2][:].bitcast(U32), slot_words, 2, 3, E, late[:, :C])
-                gather(words[LAST][:].bitcast(U32), slot_words, LAST, 3, E, late[:, C:])
-            scatter(e, e + 1, 2)
-            scatter(e, e + 1, 3)
-            layer2(e + 1)
+        hidden_quantize(1)
+        scatter("scalar", 0, 0, C, rows[:, 0])
+        scatter("scalar", 1, 0, C, rows[:, 1])
+
+        for s in range(PASSES):
+            layer1(2, s, "a0", 0, H)
+        rows = rows_tile("y_rows0_2", 2, C, tag="w1w2_2")
+        leave(0, 2, BLOCKS, rows[:])
+        late = keep.tile([P, 2 * C], U32, name="late_words", tag="h_words0", align_bytes=64)
+        gather(words[2][:].bitcast(U32), slot_words, 2, 3, E, late[:, :C])
+        gather(words[LAST][:].bitcast(U32), slot_words, LAST, 3, E, late[:, C:])
+        layer2(1, 0, BLOCKS, "v1")
+        first = rows_tile("y_rows1_0", 1, C)
+        leave(1, 0, 1, first[:])
+        scatter("vector", 2, 0, C, rows[:, 0])
+        scatter("scalar", 3, 0, C, rows[:, 1])
+        scatter("vector", 0, C, 2 * C, first[:, 0])
+        hidden(2)
+
+        for s in range(PASSES):
+            layer1(3, s, "a1", 0, H)
+        rows = rows_tile("y_rows1_1", 2, C, tag="w1w3_2")
+        hidden_quantize(2)
+        leave(1, 1, 3, rows[:])
+        scatter("scalar", 1, C, 2 * C, rows[:, 0])
+        scatter("vector", 2, C, 2 * C, rows[:, 1])
+        layer2(2, 0, BLOCKS, "s1")
         hidden(3)
-        rows = keep.tile([P, 3, 2, C], F32, name="y_rows_last", tag="h_rows3", align_bytes=64)
-        leave(2, 0, rows[:, 0])
-        leave(2, 1, rows[:, 1:, 0, :])
+
+        last = rows_tile("y_rows_last", BLOCKS, 3 * C, tag="h_rows3")
+        leave(1, 3, BLOCKS, last[:, 3:, :C])
+        leave(2, 0, BLOCKS, last[:, :, C : 2 * C])
         hidden_quantize(3)
-        y_rows[2, 0], y_rows[2, 1], y_rows[2, 3], y_rows[3, 3] = rows[:, 0, 0], rows[:, 0, 1], rows[:, 2, 0], rows[:, 2, 1]
-        y_rows[2, 2] = rows[:, 1].rearrange("p e c -> p (e c)")
-        scatter(2, 3, 0)
-        scatter(2, 3, 1)
-        scatter(2, 3, 3)
-        layer2(3)
-        leave(3, 0, rows_tile(3, E, 0)[:])
-        leave(3, 1, rows[:, 1:, 1, :])
-        scatter(3, E, 1)
-        scatter(3, E, 0)
-        scatter(3, E, 3)
-        scatter(2, E, 2)
+        scatter("scalar", 3, C, 2 * C, last[:, 3, :C])
+        scatter("vector", 0, 2 * C, 3 * C, last[:, 0, C : 2 * C])
+        scatter("scalar", 1, 2 * C, 3 * C, last[:, 1, C : 2 * C])
+        scatter("scalar", 3, 2 * C, 3 * C, last[:, 3, C : 2 * C])
+        layer2(3, 0, 2, "v0")
+        layer2(3, 2, BLOCKS, "s0")
+        leave(3, 0, 2, last[:, :2, 2 * C :])
+        leave(3, 2, BLOCKS, last[:, 2:, 2 * C :])
+        scatter("scalar", 1, 3 * C, SLOTS, last[:, 1, 2 * C :])
+        scatter("vector", 0, 3 * C, SLOTS, last[:, 0, 2 * C :])
+        scatter("scalar", 3, 3 * C, SLOTS, last[:, 3, 2 * C :])
+        scatter("vector", 2, 2 * C, SLOTS, last[:, 2, C:])

@@ -61,7 +61,12 @@ def tile_moe_pln_mlp_relu_kernel(
         words = [keep.tile([P, WINDOW], I32, name=f"words{s}", align_bytes=64) for s in range(PASSES)]
         scales = {s: keep.tile([P, WINDOW], U8, name=f"scales{s}", align_bytes=64) for s in (0, 2, 3)}
         shifted = keep.tile([P, SLOTS], U8, name="shifted", align_bytes=64)
-        w1s = [keep.tile([P, PASSES, H], U8, name=f"w1s{e}", align_bytes=64) for e in range(E)]
+        w1s = {e: keep.tile([P, PASSES, H], U8, name=f"w1s{e}", align_bytes=64) for e in range(2, E)}
+        w1s_first = keep.tile([P, LAST, H], U8, name="w1s_first", align_bytes=64)
+        w1s_second = keep.tile([P, PASSES + 1, H], U8, name="w1s_second", align_bytes=64)
+        w1_planes = {(e, s): w1s[e][:, s, :] for e in range(2, E) for s in range(PASSES)}
+        for g in range(2 * PASSES):
+            w1_planes[divmod(g, PASSES)] = w1s_first[:, g, :] if g < LAST else w1s_second[:, g - LAST, :]
         w2w = [keep.tile([P, 1, 2 * N], U8, name=f"w2w{e}", align_bytes=64) for e in range(2)]
         w2w_late = keep.tile([P, 2, 2 * N], U8, name="w2w_late", align_bytes=64)
         w2s = keep.tile([P, E, N], U8, name="w2s", align_bytes=64)
@@ -73,7 +78,7 @@ def tile_moe_pln_mlp_relu_kernel(
         nc.vector.memset(zero[:], 0.0)
         for b in range(2, BLOCKS):
             nc.scalar.activation(out=outs[b][:], in_=zero[:].to_broadcast([P, T]), func=COPY)
-        for tile in w1s[1:]:
+        for tile in (w1s_second, w1s[2], w1s[3]):
             nc.gpsimd.memset(tile[:].rearrange("p s i -> p (s i)").bitcast(I32), 0)
         make_identity(nc, ident[:])
         nc.gpsimd.memset(outs[1][:], 0.0)
@@ -81,7 +86,7 @@ def tile_moe_pln_mlp_relu_kernel(
             nc.vector.memset(words[s][:, T:WINDOW], 0)
         for tile in (scales[0], scales[2], scales[3], shifted):
             nc.vector.memset(tile[:].bitcast(I32), 0)
-        for tile in (w1s[0], w2s):
+        for tile in (w1s_first, w2s):
             nc.vector.memset(tile[:].rearrange("p s i -> p (s i)").bitcast(I32), 0)
         nc.vector.memset(outs[0][:], 0.0)
 
@@ -160,7 +165,7 @@ def tile_moe_pln_mlp_relu_kernel(
                 lhsT=slot_words[s, e].bitcast(FP8X4),
                 lhsT_scale=slot_scales[s, e],
                 rhs=w1w[e, s][:, 2 * c0 : 2 * c1].bitcast(FP4X4),
-                rhs_scale=w1s[e][:, s, c0:c1],
+                rhs_scale=w1_planes[e, s][:, c0:c1],
                 start=(s == 0),
                 stop=(s == LAST),
             )
@@ -246,14 +251,15 @@ def tile_moe_pln_mlp_relu_kernel(
             slot_scales[1, e] = shifted[:, e * C : (e + 1) * C]
         gather_words(1, 0, E)
 
-        load_scale_rows(w1s[0], w1_scales[0])
-        load_w1(0, 0, LAST)
+        scale_rows = w1_scales.rearrange("e s q i -> (e s) q i")
+        load_scale_rows(w1s_first, scale_rows[:LAST])
+        load_w1(0, 0, 2)
+        load_w1(0, 2, PASSES)
         nc.sync.dma_start(
             out=shifted[0:SCALE_SPAN, :].bitcast(I32),
             in_=packed[PACKED_ROW : PACKED_ROW + SCALE_SPAN, :].bitcast(I32),
         )
-        load_scale_rows(w1s[1], w1_scales[1])
-        load_w1(0, LAST, PASSES)
+        load_scale_rows(w1s_second, scale_rows[LAST : 2 * PASSES])
         load_w1(1, 0, 2)
         load_scale_rows(w2s, w2_scales[:, 0])
         nc.sync.dma_start(out=gates[:, : 2 * C], in_=gate[0:P, : 2 * C])
@@ -275,7 +281,7 @@ def tile_moe_pln_mlp_relu_kernel(
         round_and_quantize(LAST)
         gather_words(LAST, 0, 1)
         gather_scales(LAST, 0, 1)
-        for s in range(PASSES):
+        for s in (0, 2, 1, LAST):
             for q in range(PACK):
                 layer1(0, s, QUARTER_BANKS[q], q * P, (q + 1) * P)
         gather_words(2, 1, 2, tag="grouped3_512")
@@ -288,14 +294,14 @@ def tile_moe_pln_mlp_relu_kernel(
         for s in range(PASSES):
             layer1(1, s, "a1", 0, H)
         hidden_quantize(0)
-        gather_scales(LAST, 2, E, tag="h_grouped0")
+        gather_words(LAST, 2, 3, tag="h_grouped0")
 
         layer2(0, 0, 2, "v0")
         layer2(0, 2, BLOCKS, "s0")
         hidden(1)
         rows = rows_tile("y_rows0_0", 2, C)
         leave(0, 0, 2, rows[:])
-        gather_words(LAST, 2, 3, tag="h_words0")
+        gather_scales(LAST, 2, E, tag="h_scales0")
         hidden_quantize(1)
         scatter("scalar", 0, 0, C, rows[:, 0])
         scatter("scalar", 1, 0, C, rows[:, 1])
@@ -304,7 +310,7 @@ def tile_moe_pln_mlp_relu_kernel(
             layer1(2, s, "a0", 0, H)
         rows = rows_tile("y_rows0_2", 2, C, tag="w1w2_2")
         leave(0, 2, BLOCKS, rows[:])
-        late = keep.tile([P, 2 * C], U32, name="late_words", tag="h_words0", align_bytes=64)
+        late = keep.tile([P, 2 * C], U32, name="late_words", tag="h_grouped0", align_bytes=64)
         gather(words[2][:].bitcast(U32), slot_words, 2, 3, E, late[:, :C])
         gather(words[LAST][:].bitcast(U32), slot_words, LAST, 3, E, late[:, C:])
         layer2(1, 0, BLOCKS, "v1")

@@ -44,6 +44,7 @@ QUANTS = (
     ((0, 256), (256, 512), (512, 640)),
     ((0, 256), (256, 512), (512, 640)),
 )
+SCALE_GROUPS = ((0, 3), (3, 8), (8, 14), (14, 16))
 QUARTER_BANKS = ("a0", "v1", "s1", "t1")
 
 
@@ -61,12 +62,11 @@ def tile_moe_pln_mlp_relu_kernel(
         words = [keep.tile([P, WINDOW], I32, name=f"words{s}", align_bytes=64) for s in range(PASSES)]
         scales = {s: keep.tile([P, WINDOW], U8, name=f"scales{s}", align_bytes=64) for s in (0, 2, 3)}
         shifted = keep.tile([P, SLOTS], U8, name="shifted", align_bytes=64)
-        w1s = {e: keep.tile([P, PASSES, H], U8, name=f"w1s{e}", align_bytes=64) for e in range(2, E)}
-        w1s_first = keep.tile([P, LAST, H], U8, name="w1s_first", align_bytes=64)
-        w1s_second = keep.tile([P, PASSES + 1, H], U8, name="w1s_second", align_bytes=64)
-        w1_planes = {(e, s): w1s[e][:, s, :] for e in range(2, E) for s in range(PASSES)}
-        for g in range(2 * PASSES):
-            w1_planes[divmod(g, PASSES)] = w1s_first[:, g, :] if g < LAST else w1s_second[:, g - LAST, :]
+        w1s, w1_planes = [], {}
+        for g0, g1 in SCALE_GROUPS:
+            w1s.append(keep.tile([P, g1 - g0, H], U8, name=f"w1s{g0}", align_bytes=64))
+            for g in range(g0, g1):
+                w1_planes[divmod(g, PASSES)] = w1s[-1][:, g - g0, :]
         w2w = [keep.tile([P, 1, 2 * N], U8, name=f"w2w{e}", align_bytes=64) for e in range(2)]
         w2w_late = keep.tile([P, 2, 2 * N], U8, name="w2w_late", align_bytes=64)
         w2s = keep.tile([P, E, N], U8, name="w2s", align_bytes=64)
@@ -78,7 +78,7 @@ def tile_moe_pln_mlp_relu_kernel(
         nc.vector.memset(zero[:], 0.0)
         for b in range(2, BLOCKS):
             nc.scalar.activation(out=outs[b][:], in_=zero[:].to_broadcast([P, T]), func=COPY)
-        for tile in (w1s_second, w1s[2], w1s[3]):
+        for tile in w1s[1:]:
             nc.gpsimd.memset(tile[:].rearrange("p s i -> p (s i)").bitcast(I32), 0)
         make_identity(nc, ident[:])
         nc.gpsimd.memset(outs[1][:], 0.0)
@@ -86,7 +86,7 @@ def tile_moe_pln_mlp_relu_kernel(
             nc.vector.memset(words[s][:, T:WINDOW], 0)
         for tile in (scales[0], scales[2], scales[3], shifted):
             nc.vector.memset(tile[:].bitcast(I32), 0)
-        for tile in (w1s_first, w2s):
+        for tile in (w1s[0], w2s):
             nc.vector.memset(tile[:].rearrange("p s i -> p (s i)").bitcast(I32), 0)
         nc.vector.memset(outs[0][:], 0.0)
 
@@ -182,6 +182,10 @@ def tile_moe_pln_mlp_relu_kernel(
                         in_=a_sums[e, q * P][:].rearrange("p (m u v) -> p u m v", u=2, v=2),
                         func=RELU,
                     )
+            elif e == 2:
+                nc.scalar.activation(
+                    out=halves, in_=a_sums[e, 0][:].rearrange("p (m u v) -> p u m v", u=2, v=2), func=RELU
+                )
             else:
                 for u in range(2):
                     nc.scalar.activation(
@@ -252,25 +256,29 @@ def tile_moe_pln_mlp_relu_kernel(
         gather_words(1, 0, E)
 
         scale_rows = w1_scales.rearrange("e s q i -> (e s) q i")
-        load_scale_rows(w1s_first, scale_rows[:LAST])
+
+        def load_group(n):
+            load_scale_rows(w1s[n], scale_rows[SCALE_GROUPS[n][0] : SCALE_GROUPS[n][1]])
+
+        load_group(0)
         load_w1(0, 0, 2)
         load_w1(0, 2, PASSES)
         nc.sync.dma_start(
             out=shifted[0:SCALE_SPAN, :].bitcast(I32),
             in_=packed[PACKED_ROW : PACKED_ROW + SCALE_SPAN, :].bitcast(I32),
         )
-        load_scale_rows(w1s_second, scale_rows[LAST : 2 * PASSES])
+        load_group(1)
         load_w1(1, 0, 2)
         load_scale_rows(w2s, w2_scales[:, 0])
         nc.sync.dma_start(out=gates[:, : 2 * C], in_=gate[0:P, : 2 * C])
         load_w1(1, 2, PASSES)
         load_words(w2w[0], w2_words[0])
-        load_scale_rows(w1s[2], w1_scales[2])
+        load_group(2)
         load_w1(2, 0, 2)
         load_w1(2, 2, PASSES)
         load_words(w2w[1], w2_words[1])
-        load_scale_rows(w1s[3], w1_scales[3])
         load_w1(3, 0, 2)
+        load_group(3)
         load_w1(3, 2, PASSES)
         load_words(w2w_late, w2_words[2:E, 0])
         nc.sync.dma_start(out=gates[:, 2 * C :], in_=gate[0:P, 2 * C :])
@@ -302,26 +310,30 @@ def tile_moe_pln_mlp_relu_kernel(
         rows = rows_tile("y_rows0_0", 2, C)
         leave(0, 0, 2, rows[:])
         gather_scales(LAST, 2, E, tag="h_scales0")
-        hidden_quantize(1)
         scatter("scalar", 0, 0, C, rows[:, 0])
         scatter("scalar", 1, 0, C, rows[:, 1])
+        rows = rows_tile("y_rows0_2", 1, C, tag="h_rows1")
+        leave(0, 2, 3, rows[:])
+        hidden_quantize(1)
+        scatter("vector", 2, 0, C, rows[:, 0])
 
         for s in range(PASSES):
             layer1(2, s, "a0", 0, H)
-        rows = rows_tile("y_rows0_2", 2, C, tag="w1w2_2")
-        leave(0, 2, BLOCKS, rows[:])
+        rows = rows_tile("y_rows0_3", 1, C, tag="w1w2_2")
+        leave(0, 3, BLOCKS, rows[:])
         late = keep.tile([P, 2 * C], U32, name="late_words", tag="h_grouped0", align_bytes=64)
         gather(words[2][:].bitcast(U32), slot_words, 2, 3, E, late[:, :C])
         gather(words[LAST][:].bitcast(U32), slot_words, LAST, 3, E, late[:, C:])
         layer2(1, 0, BLOCKS, "v1")
+        for s in range(2):
+            layer1(3, s, "a1", 0, H)
         first = rows_tile("y_rows1_0", 1, C)
         leave(1, 0, 1, first[:])
-        scatter("vector", 2, 0, C, rows[:, 0])
-        scatter("scalar", 3, 0, C, rows[:, 1])
+        scatter("scalar", 3, 0, C, rows[:, 0])
         scatter("vector", 0, C, 2 * C, first[:, 0])
         hidden(2)
 
-        for s in range(PASSES):
+        for s in range(2, PASSES):
             layer1(3, s, "a1", 0, H)
         rows = rows_tile("y_rows1_1", 2, C, tag="w1w3_2")
         hidden_quantize(2)

from contextlib import ExitStack

import concourse.mybir as mybir
from concourse.masks import make_identity

K, T, E, C, H, N = 2048, 640, 4, 128, 512, 512
SLOTS = E * C
FLOPS = 2 * SLOTS * H * (K + N)

P = 128
PACK = 4
K_PASS = P * PACK
PASSES = K // K_PASS
LAST = PASSES - 1
WINDOW = 704
LIST_COLS = C // 16
BLOCKS = N // P
QUADRANT = 32
PACKED_ROW = 4
SCALE_SPAN = 3 * QUADRANT + 4
RUN = 4

F32 = mybir.dt.float32
BF16 = mybir.dt.bfloat16
I32 = mybir.dt.int32
U32 = mybir.dt.uint32
U16 = mybir.dt.uint16
U8 = mybir.dt.uint8
FP8X4 = mybir.dt.float8_e4m3fn_x4
FP4X4 = mybir.dt.float4_e2m1fn_x4
COPY = mybir.ActivationFunctionType.Copy
RELU = mybir.ActivationFunctionType.Relu
MULT = mybir.AluOpType.mult

CASTS = (
    ((0, 256, "vector"), (256, 384, "vector"), (384, 640, "scalar")),
    ((0, 256, "vector"), (256, 384, "vector"), (384, 512, "scalar"), (512, 640, "scalar")),
    ((0, 256, "scalar"), (256, 384, "scalar"), (384, 512, "gpsimd"), (512, 640, "scalar")),
    ((0, 128, "scalar"), (128, 256, "vector"), (256, 384, "vector"), (384, 512, "scalar"), (512, 640, "scalar")),
)
QUANTS = (
    ((0, 256), (256, 384), (384, 640)),
    ((384, 512), (0, 256), (256, 384), (512, 640)),
    ((0, 256), (256, 512), (512, 640)),
    ((0, 256), (256, 512), (512, 640)),
)
SCALE_GROUPS = ((0, 3), (3, 8), (8, 14), (14, 16))
QUARTER_BANKS = ("a0", "v1", "s1", "t1")


def tile_moe_pln_mlp_relu_kernel(
    tc, xT, w1_words, w1_scales, w2_words, w2_scales, gate, offs, out
):
    nc = tc.nc
    with ExitStack() as ctx:
        keep = ctx.enter_context(tc.tile_pool(name="keep", bufs=1))
        psum = ctx.enter_context(tc.psum_pool(name="psum", bufs=1))

        offsets = keep.tile([P, SLOTS // 16], U16, name="offsets")

        raw = [keep.tile([P, PACK, T], F32, name=f"raw{s}", align_bytes=64) for s in range(PASSES)]
        words = [keep.tile([P, WINDOW], I32, name=f"words{s}", align_bytes=64) for s in range(PASSES)]
        scales = {s: keep.tile([P, WINDOW], U8, name=f"scales{s}", align_bytes=64) for s in (0, 2, 3)}
        shifted = keep.tile([P, SLOTS], U8, name="shifted", align_bytes=64)
        w1s, w1_planes = [], {}
        for g0, g1 in SCALE_GROUPS:
            w1s.append(keep.tile([P, g1 - g0, H], U8, name=f"w1s{g0}", align_bytes=64))
            for g in range(g0, g1):
                w1_planes[divmod(g, PASSES)] = w1s[-1][:, g - g0, :]
        w2w = [keep.tile([P, 1, 2 * N], U8, name=f"w2w{e}", align_bytes=64) for e in range(2)]
        w2w_late = keep.tile([P, 2, 2 * N], U8, name="w2w_late", align_bytes=64)
        w2s = keep.tile([P, E, N], U8, name="w2s", align_bytes=64)
        outs = [keep.tile([P, T], F32, name=f"outs{b}") for b in range(BLOCKS)]
        ident = keep.tile([P, P], F32, name="ident")
        zero = keep.tile([P, 1], F32, name="zero")
        gates = keep.tile([P, SLOTS], F32, name="gates")

        nc.vector.memset(zero[:], 0.0)
        for b in range(2, BLOCKS):
            nc.scalar.activation(out=outs[b][:], in_=zero[:].to_broadcast([P, T]), func=COPY)
        for tile in w1s[1:]:
            nc.gpsimd.memset(tile[:].rearrange("p s i -> p (s i)").bitcast(I32), 0)
        make_identity(nc, ident[:])
        nc.gpsimd.memset(outs[1][:], 0.0)
        for s in range(PASSES):
            nc.vector.memset(words[s][:, T:WINDOW], 0)
        for tile in (scales[0], scales[2], scales[3], shifted):
            nc.vector.memset(tile[:].bitcast(I32), 0)
        for tile in (w1s[0], w2s):
            nc.vector.memset(tile[:].rearrange("p s i -> p (s i)").bitcast(I32), 0)
        nc.vector.memset(outs[0][:], 0.0)

        def load_scale_rows(tile, rows):
            for r in range(4):
                nc.sync.dma_start(
                    out=tile[r:P:QUADRANT, :, :].bitcast(I32),
                    in_=rows[:, r:16:4, :].rearrange("g q i -> q g i").bitcast(I32),
                )

        def load_words(tile, rows):
            nc.sync.dma_start(out=tile[:].bitcast(I32), in_=rows.rearrange("g p c -> p g c").bitcast(I32))

        w1w = {}

        def load_w1(e, s0, s1):
            tile = keep.tile([P, s1 - s0, 2 * H], U8, name=f"w1w{e}_{s0}", align_bytes=64)
            load_words(tile, w1_words[e, s0:s1])
            for s in range(s0, s1):
                w1w[e, s] = tile[:, s - s0, :]

        for s in range(PASSES):
            nc.sync.dma_start(
                out=raw[s][:], in_=xT[s * K_PASS : (s + 1) * K_PASS, :].rearrange("(p j) t -> p j t", j=PACK)
            )
            if s == 0:
                nc.sync.dma_start(offsets[:], offs)

        grouped = {}

        def round_and_quantize(s):
            for q0, q1 in QUANTS[s]:
                grouped[s, q0] = keep.tile([P, (q1 - q0) * PACK], BF16, name=f"grouped{s}_{q0}", align_bytes=64)
            for t0, t1, engine in CASTS[s]:
                q0 = [a for a, b in QUANTS[s] if a <= t0 and t1 <= b][0]
                dst = grouped[s, q0][:, (t0 - q0) * PACK : (t1 - q0) * PACK].rearrange("p (c i t) -> p c t i", i=RUN, t=PACK)
                src = raw[s][:, :, t0:t1].rearrange("p t (c i) -> p c t i", i=RUN)
                if engine == "vector":
                    nc.vector.tensor_copy(out=dst, in_=src)
                elif engine == "gpsimd":
                    nc.gpsimd.tensor_copy(out=dst, in_=src)
                else:
                    nc.scalar.activation(out=dst, in_=src, func=COPY)
            for t0, t1 in QUANTS[s]:
                nc.vector.quantize_mx(
                    out=words[s][:, t0:t1].bitcast(FP8X4),
                    scales=scales[0][PACKED_ROW:P, t0:t1] if s == 1 else scales[s][:, t0:t1],
                    in_=grouped[s, t0][:],
                )

        slot_words, slot_scales = {}, {}

        def gather(window, found, s, e0, e1, dst):
            nc.vector.tensor_copy(out=dst, in_=window.indirect(offsets[:, e0 * LIST_COLS : e1 * LIST_COLS]))
            for e in range(e0, e1):
                found[s, e] = dst[:, (e - e0) * C : (e - e0 + 1) * C]

        def gather_words(s, e0, e1, tag=None):
            name = f"slot_words{s}_{e0}"
            dst = keep.tile([P, (e1 - e0) * C], U32, name=name, tag=tag or name, align_bytes=64)
            gather(words[s][:].bitcast(U32), slot_words, s, e0, e1, dst[:])

        def gather_scales(s, e0, e1, tag=None):
            name = f"slot_scales{s}_{e0}"
            dst = keep.tile([P, (e1 - e0) * C], U8, name=name, tag=tag or name, align_bytes=64)
            gather(scales[s][:], slot_scales, s, e0, e1, dst[:])
            return dst

        a_sums = {}

        def layer1(e, s, bank, c0, c1):
            if s == 0:
                a_sums[e, c0] = psum.tile([P, c1 - c0], F32, name=f"a{e}_{c0}", tag=bank)
            nc.tensor.matmul_mx(
                out=a_sums[e, c0][:],
                lhsT=slot_words[s, e].bitcast(FP8X4),
                lhsT_scale=slot_scales[s, e],
                rhs=w1w[e, s][:, 2 * c0 : 2 * c1].bitcast(FP4X4),
                rhs_scale=w1_planes[e, s][:, c0:c1],
                start=(s == 0),
                stop=(s == LAST),
            )

        h_grouped, h_words, h_scales = {}, {}, {}

        def hidden(e):
            h_rows = keep.tile([P, H], BF16, name=f"h_rows{e}", align_bytes=64)
            halves = h_rows[:].rearrange("p (u m v) -> p u m v", u=2, v=2)
            if e == 0:
                for q in range(PACK):
                    nc.scalar.activation(
                        out=halves[:, :, q * QUADRANT : (q + 1) * QUADRANT, :],
                        in_=a_sums[e, q * P][:].rearrange("p (m u v) -> p u m v", u=2, v=2),
                        func=RELU,
                    )
            elif e == 2:
                nc.scalar.activation(
                    out=halves, in_=a_sums[e, 0][:].rearrange("p (m u v) -> p u m v", u=2, v=2), func=RELU
                )
            else:
                for u in range(2):
                    nc.scalar.activation(
                        out=halves[:, u],
                        in_=a_sums[e, 0][:].rearrange("p (m u v) -> p u m v", u=2, v=2)[:, u],
                        func=RELU,
                    )
            turned = psum.tile([P, 2, C], F32, name=f"turned{e}", tag=f"t{e % 2}")
            pairs = h_rows[:].bitcast(F32)
            for u in range(2):
                nc.tensor.transpose(turned[:, u, :], pairs[:, u * P : (u + 1) * P], ident[:])
            h_grouped[e] = keep.tile([P, 2 * C], F32, name=f"h_grouped{e}", align_bytes=64)
            copy = nc.vector.tensor_copy if e == 1 else nc.scalar.copy
            copy(out=h_grouped[e][:].rearrange("p (c u) -> p c u", u=2), in_=turned[:].rearrange("p u c -> p c u"))

        def hidden_quantize(e, tag=None):
            h_words[e] = keep.tile([P, C], U32, name=f"h_words{e}", tag=tag or f"h_words{e}", align_bytes=64)
            h_scales[e] = keep.tile([P, C], U8, name=f"h_scales{e}", align_bytes=64)
            nc.vector.quantize_mx(
                out=h_words[e][:].bitcast(FP8X4), scales=h_scales[e][:], in_=h_grouped[e][:].bitcast(BF16)
            )

        y_sums = {}

        def layer2(e, b0, b1, bank):
            w2 = w2w[e][:, 0, :] if e < 2 else w2w_late[:, e - 2, :]
            sums = psum.tile([P, b1 - b0, C], F32, name=f"y{e}_{b0}", tag=bank)
            for b in range(b0, b1):
                y_sums[e, b] = (sums, b - b0)
                nc.tensor.matmul_mx(
                    out=sums[:, b - b0, :],
                    lhsT=w2[:, b * 2 * P : (b + 1) * 2 * P].bitcast(FP4X4),
                    lhsT_scale=w2s[:, e, b * P : (b + 1) * P],
                    rhs=h_words[e][:].bitcast(FP8X4),
                    rhs_scale=h_scales[e][:],
                    start=True,
                    stop=True,
                )

        def leave(e, b0, b1, rows):
            sums, i = y_sums[e, b0]
            nc.vector.tensor_tensor(
                rows,
                sums[:, i : i + b1 - b0, :],
                gates[:, e * C : (e + 1) * C].unsqueeze(1).to_broadcast([P, b1 - b0, C]),
                MULT,
            )

        def rows_tile(name, blocks, slots, tag=None):
            return keep.tile([P, blocks, slots], F32, name=name, tag=tag or name, align_bytes=64)

        def scatter(engine, b, j0, j1, rows):
            window = outs[b][:].indirect(offsets[:, j0 // 16 : j1 // 16])
            if engine == "vector":
                nc.vector.tensor_copy(out=window, in_=rows)
            else:
                nc.scalar.activation(out=window, in_=rows, func=COPY)
            if j1 == SLOTS:
                nc.sync.dma_start(out=out[b * P : (b + 1) * P, :], in_=outs[b][:])

        round_and_quantize(0)
        gather_words(0, 0, E - 1)
        round_and_quantize(1)
        gather_words(0, E - 1, E, tag="grouped1_256")
        packed = gather_scales(0, 0, E)
        for e in range(E):
            slot_scales[1, e] = shifted[:, e * C : (e + 1) * C]
        gather_words(1, 0, E)

        scale_rows = w1_scales.rearrange("e s q i -> (e s) q i")

        def load_group(n):
            load_scale_rows(w1s[n], scale_rows[SCALE_GROUPS[n][0] : SCALE_GROUPS[n][1]])

        load_group(0)
        load_w1(0, 0, 2)
        load_w1(0, 2, PASSES)
        nc.sync.dma_start(
            out=shifted[0:SCALE_SPAN, :].bitcast(I32),
            in_=packed[PACKED_ROW : PACKED_ROW + SCALE_SPAN, :].bitcast(I32),
        )
        load_group(1)
        load_w1(1, 0, 2)
        load_scale_rows(w2s, w2_scales[:, 0])
        nc.sync.dma_start(out=gates[:, : 2 * C], in_=gate[0:P, : 2 * C])
        load_w1(1, 2, PASSES)
        load_words(w2w[0], w2_words[0])
        load_group(2)
        load_w1(2, 0, 2)
        load_w1(2, 2, PASSES)
        load_words(w2w[1], w2_words[1])
        load_w1(3, 0, 2)
        load_group(3)
        load_w1(3, 2, PASSES)
        load_words(w2w_late, w2_words[2:E, 0])
        nc.sync.dma_start(out=gates[:, 2 * C :], in_=gate[0:P, 2 * C :])

        round_and_quantize(2)
        gather_words(2, 0, 1)
        gather_scales(2, 0, 1)
        round_and_quantize(LAST)
        gather_words(LAST, 0, 1)
        gather_scales(LAST, 0, 1)
        for s in (0, 2, 1, LAST):
            for q in range(PACK):
                layer1(0, s, QUARTER_BANKS[q], q * P, (q + 1) * P)
        gather_words(2, 1, 2, tag="grouped3_512")
        gather_words(LAST, 1, 2)
        gather_scales(LAST, 1, 2)
        gather_scales(2, 1, 2, tag="slot_words3_0")
        gather_scales(2, 2, E, tag="slot_scales3_0")
        hidden(0)
        gather_words(2, 2, 3, tag="h_rows0")
        for s in range(PASSES):
            layer1(1, s, "a1", 0, H)
        hidden_quantize(0)
        gather_words(LAST, 2, 3, tag="h_grouped0")

        layer2(0, 0, 2, "v0")
        layer2(0, 2, BLOCKS, "s0")
        hidden(1)
        rows = rows_tile("y_rows0_0", 2, C)
        leave(0, 0, 2, rows[:])
        gather_scales(LAST, 2, E, tag="h_scales0")
        scatter("scalar", 0, 0, C, rows[:, 0])
        scatter("scalar", 1, 0, C, rows[:, 1])
        rows = rows_tile("y_rows0_2", 1, C, tag="h_rows1")
        leave(0, 2, 3, rows[:])
        hidden_quantize(1)
        scatter("vector", 2, 0, C, rows[:, 0])

        for s in range(PASSES):
            layer1(2, s, "a0", 0, H)
        rows = rows_tile("y_rows0_3", 1, C, tag="w1w2_2")
        leave(0, 3, BLOCKS, rows[:])
        late = keep.tile([P, 2 * C], U32, name="late_words", tag="h_grouped0", align_bytes=64)
        gather(words[2][:].bitcast(U32), slot_words, 2, 3, E, late[:, :C])
        gather(words[LAST][:].bitcast(U32), slot_words, LAST, 3, E, late[:, C:])
        layer2(1, 0, BLOCKS, "v1")
        for s in range(2):
            layer1(3, s, "a1", 0, H)
        first = rows_tile("y_rows1_0", 1, C)
        leave(1, 0, 1, first[:])
        scatter("scalar", 3, 0, C, rows[:, 0])
        scatter("vector", 0, C, 2 * C, first[:, 0])
        hidden(2)

        for s in range(2, PASSES):
            layer1(3, s, "a1", 0, H)
        rows = rows_tile("y_rows1_1", 2, C, tag="w1w3_2")
        hidden_quantize(2)
        leave(1, 1, 3, rows[:])
        scatter("scalar", 1, C, 2 * C, rows[:, 0])
        scatter("vector", 2, C, 2 * C, rows[:, 1])
        layer2(2, 0, BLOCKS, "s1")
        hidden(3)

        last = rows_tile("y_rows_last", BLOCKS, 3 * C, tag="h_rows3")
        leave(1, 3, BLOCKS, last[:, 3:, :C])
        leave(2, 0, BLOCKS, last[:, :, C : 2 * C])
        hidden_quantize(3)
        scatter("scalar", 3, C, 2 * C, last[:, 3, :C])
        scatter("vector", 0, 2 * C, 3 * C, last[:, 0, C : 2 * C])
        scatter("scalar", 1, 2 * C, 3 * C, last[:, 1, C : 2 * C])
        scatter("scalar", 3, 2 * C, 3 * C, last[:, 3, C : 2 * C])
        layer2(3, 0, 2, "v0")
        layer2(3, 2, BLOCKS, "s0")
        leave(3, 0, 2, last[:, :2, 2 * C :])
        leave(3, 2, BLOCKS, last[:, 2:, 2 * C :])
        scatter("scalar", 1, 3 * C, SLOTS, last[:, 1, 2 * C :])
        scatter("vector", 0, 3 * C, SLOTS, last[:, 0, 2 * C :])
        scatter("scalar", 3, 3 * C, SLOTS, last[:, 3, 2 * C :])
        scatter("vector", 2, 2 * C, SLOTS, last[:, 2, C:])
